import numpy as np
import ml_dtypes


def mxq(x, axis, fmt="e4m3"):
    dtype, down = {"e4m3": (ml_dtypes.float8_e4m3fn, 7), "e5m2": (ml_dtypes.float8_e5m2, 14)}[fmt]
    v = np.moveaxis(np.asarray(x, np.float32).astype(ml_dtypes.bfloat16).astype(np.float64), axis, -1)
    blocks = v.reshape(v.shape[:-1] + (-1, 32))
    amax = np.abs(blocks).max(-1, keepdims=True)
    byte = np.maximum(np.where(amax > 0, np.frexp(amax)[1] - 1 + 127, 0) - down, 1)
    scale = np.exp2(byte - 127.0)
    codes = (blocks / scale).astype(np.float32).astype(dtype).astype(np.float64)
    return np.moveaxis((codes * scale).reshape(v.shape), -1, axis)


WIDE = False


def mx_kscale(k):
    if not WIDE:
        return np.ones(k)
    levels = np.array([10, -10, 5, -5, 0])
    if k % 512:
        return np.exp2(np.random.permutation(np.resize(levels, k // 32))).repeat(32)
    a = np.empty((k // 512, 16))
    for p in range(k // 512):
        a[p, :8] = np.random.permutation(np.resize(levels, 8))
        for g in range(8):
            far = levels[np.abs(levels - a[p, g]) >= 10]
            a[p, g + 8] = far[np.random.randint(len(far))]
    return np.exp2(a.ravel()).repeat(32)


def f64(x):
    return np.asarray(x).astype(np.float64)


def striped(idx):
    return np.tile(idx.reshape(-1, 16).T, (8, 1)).astype(np.uint16)


def unstriped(offs):
    return offs[:16].T.reshape(-1).astype(np.int64)


E2M1 = np.array([0.0, 0.5, 1.0, 1.5, 2.0, 3.0, 4.0, 6.0, -0.0, -0.5, -1.0, -1.5, -2.0, -3.0, -4.0, -6.0])


def pack_fp4(w):
    k, n = w.shape
    w = f64(np.asarray(w, np.float32).astype(ml_dtypes.bfloat16)).reshape(k // 32, 32, n)
    amax = np.abs(w).max(1)
    mant, ex = np.frexp(amax / 6.0)
    byte = np.clip(np.where(amax > 0, np.where(mant > 0.5, ex, ex - 1) + 127, 1), 1, 254)
    scaled = (w * np.exp2(127.0 - byte)[:, None, :]).reshape(k, n).astype(np.float32)
    c = np.ascontiguousarray(scaled.reshape(k // 512, 128, 4, n).transpose(0, 1, 3, 2)).astype(ml_dtypes.float4_e2m1fn).view(np.uint8) & 0xF
    words = (c[..., 0::2] | (c[..., 1::2] << 4)).reshape(k // 512, 128, 2 * n)
    return np.ascontiguousarray(words), np.ascontiguousarray(byte.astype(np.uint8).reshape(k // 512, 16, n))


def unpack_fp4(words, scales):
    g, _, n = scales.shape
    words = np.ascontiguousarray(words).reshape(g, 128, n, 2)
    nib = np.empty((g, 128, n, 4), np.uint8)
    nib[..., 0::2] = words & 0xF
    nib[..., 1::2] = words >> 4
    vals = E2M1[nib] * np.repeat(np.exp2(scales.astype(np.float64) - 127.0), 8, axis=1)[..., None]
    return vals.transpose(0, 1, 3, 2).reshape(g * 512, n)


def gelu(v):
    return 0.5 * v * (1.0 + np.tanh(np.sqrt(2.0 / np.pi) * (v + 0.044715 * v**3)))


K, T, S, H, N = 1024, 2048, 512, 512, 128


def setup_inputs():
    n = np.random.standard_normal
    s = mx_kscale(K)[:, None]
    u = mx_kscale(H)
    packed_xT = pack_fp4(n((K, T)) * s)
    return {
        "x_words": packed_xT[0],
        "x_scales": packed_xT[1],
        "w1": (n((K, H)) / np.sqrt(K) / s * u).astype(np.float32),
        "w2": (n((H, N)) / np.sqrt(H) / u[:, None]).astype(np.float32),
        "pe": (0.5 * n((H, T)) * u[:, None]).astype(np.float32),
        "offs": striped(np.random.permutation(T)[:S]),
    }


def reference(x_words, x_scales, w1, w2, pe, offs):
    xq = unpack_fp4(x_words, x_scales)[:, unstriped(offs)]
    g = f64(pe)[:, unstriped(offs)]
    h = gelu((mxq(f64(w1), 0, "e4m3").T @ xq) + g)
    return mxq(f64(w2), 0, "e4m3").T @ mxq(h, 0, "e4m3")

@@ -1,0 +1,130 @@
+from contextlib import ExitStack
+
+import concourse.mybir as mybir
+
+K, T, S, H, N = 1024, 2048, 512, 512, 128
+FLOPS = 2 * S * H * (K + N)
+
+F32 = mybir.dt.float32
+BF16 = mybir.dt.bfloat16
+I32 = mybir.dt.int32
+U32 = mybir.dt.uint32
+U16 = mybir.dt.uint16
+U8 = mybir.dt.uint8
+FP8X4 = mybir.dt.float8_e4m3fn_x4
+FP4X4 = mybir.dt.float4_e2m1fn_x4
+GELU = mybir.ActivationFunctionType.Gelu_apprx_tanh
+ADD = mybir.AluOpType.add
+
+P = 128
+PACK = 4
+K_PASS = P * PACK
+PASSES = K // K_PASS
+WIDTHS = (64, 128, 128, 128, 64)
+STARTS = tuple(sum(WIDTHS[:c]) for c in range(len(WIDTHS)))
+
+
+def tile_picked_posadd_gelu_p_kernel(tc, x_words, x_scales, w1, w2, pe, offs, out):
+    nc = tc.nc
+    with ExitStack() as ctx:
+        sb = ctx.enter_context(tc.tile_pool(name="sb", bufs=1))
+        ps = ctx.enter_context(tc.psum_pool(name="ps", bufs=1))
+
+        offsets = sb.tile([P, S // 16], U16, name="offsets")
+        nc.sync.dma_start(offsets[:], offs)
+
+        scale_table = sb.tile([P, T], U8, name="scale_table", tag="slot0", align_bytes=64)
+        nc.vector.memset(scale_table[:].bitcast(I32), 0)
+        scale_rows = x_scales.rearrange("z (q r) c -> r q z c", r=4)
+
+        w1_raw = [sb.tile([P, PACK, H], F32, name=f"w1_raw{z}", tag=("w1_first", "slot2")[z], align_bytes=64) for z in range(PASSES)]
+        word_table = [sb.tile([P, T], U16, name=f"word_table{z}", tag=f"slot{2 * z + 1}", align_bytes=64) for z in range(PASSES)]
+        nc.sync.dma_start(w1_raw[0][:], w1[0:K_PASS, :].rearrange("(p j) c -> p j c", j=PACK))
+        for r in range(4):
+            nc.sync.dma_start(scale_table[r:P:16, :].bitcast(I32), scale_rows[r].bitcast(I32))
+        nc.sync.dma_start(word_table[0][:].bitcast(I32), x_words[0].bitcast(I32))
+        nc.sync.dma_start(w1_raw[1][:], w1[K_PASS:K, :].rearrange("(p j) c -> p j c", j=PACK))
+        nc.sync.dma_start(word_table[1][:].bitcast(I32), x_words[1].bitcast(I32))
+        w2_raw = sb.tile([P, PACK, N], F32, name="w2_raw", align_bytes=64)
+        nc.sync.dma_start(w2_raw[:], w2.rearrange("(p j) c -> p j c", j=PACK))
+
+        x_scale = [sb.tile([P, S], U8, name=f"x_scale{z}", align_bytes=64) for z in range(PASSES)]
+        nc.vector.memset(x_scale[1][96:P, :].bitcast(I32), 0)
+        nc.vector.tensor_copy(x_scale[0][:], scale_table[:].indirect(offsets[:]))
+        nc.sync.dma_start(x_scale[1][0 : P - 16, :].bitcast(I32), x_scale[0][16:P, :].bitcast(I32))
+        pe_rows = pe.rearrange("(p t) c -> t p c", t=PACK)
+        pe_table = []
+
+        acc = [ps.tile([P, S], F32, name=f"acc{t}", tag=f"bank{t}") for t in range(PACK)]
+        for z in range(PASSES):
+            grouped = [sb.tile([P, 2, P, PACK], BF16, name=f"w1_grouped{z}{u}", align_bytes=64) for u in range(2)]
+            src = w1_raw[z][:].rearrange("p j (m t) -> p m t j", t=PACK)
+            nc.vector.tensor_copy(grouped[0][:].rearrange("p t m j -> p m t j"), src[:, :, 0:2, :])
+            nc.scalar.copy(grouped[1][:].rearrange("p t m j -> p m t j"), src[:, :, 2:4, :])
+            x_code = sb.tile([P, S], U16, name=f"x_code{z}", align_bytes=64)
+            nc.vector.tensor_copy(x_code[:], word_table[z][:].indirect(offsets[:]))
+            for t in (2 * z, 2 * z + 1):
+                pe_table.append(sb.tile([P, T], F32, name=f"pe_table{t}", tag=f"slot{t}", align_bytes=64))
+                nc.sync.dma_start(pe_table[t][:], pe_rows[t])
+            for u in range(2):
+                codes = sb.tile([P, 2 * P], U32, name=f"w1_codes{z}{u}", align_bytes=64)
+                scales = sb.tile([P, 2 * P], U8, name=f"w1_scales{z}{u}", align_bytes=64)
+                nc.vector.quantize_mx(codes[:].bitcast(FP8X4), scales[:], grouped[u][:].rearrange("p t m j -> p (t m j)"))
+                for v in range(2):
+                    cols = slice(v * P, (v + 1) * P)
+                    nc.tensor.matmul_mx(
+                        acc[2 * u + v][:],
+                        lhsT=codes[:, cols].bitcast(FP8X4),
+                        lhsT_scale=scales[:, cols],
+                        rhs=x_code[:].bitcast(FP4X4),
+                        rhs_scale=x_scale[z][:],
+                        start=(z == 0),
+                        stop=(z == PASSES - 1),
+                    )
+
+        w2_grouped = sb.tile([P, N, PACK], BF16, name="w2_grouped", align_bytes=64)
+        nc.vector.tensor_copy(w2_grouped[:], w2_raw[:].rearrange("p j c -> p c j"))
+        w2_codes = sb.tile([P, N], U32, name="w2_codes", align_bytes=64)
+        w2_scales = sb.tile([P, N], U8, name="w2_scales", align_bytes=64)
+        nc.vector.quantize_mx(w2_codes[:].bitcast(FP8X4), w2_scales[:], w2_grouped[:].rearrange("p c j -> p (c j)"))
+
+        proj = [sb.tile([P, S], F32, name=f"proj{t}", align_bytes=64) for t in range(PACK)]
+        for t in range(PACK):
+            nc.scalar.copy(proj[t][:], acc[t][:])
+
+        chunks = [slice(a, a + w) for a, w in zip(STARTS, WIDTHS)]
+        hidden = [sb.tile([P, w, PACK], BF16, name=f"hidden{c}", align_bytes=64) for c, w in enumerate(WIDTHS)]
+        early = sb.tile([P, 2, S], F32, name="early", align_bytes=64)
+        for t in range(2):
+            nc.vector.tensor_tensor(early[:, t, :], pe_table[t][:].indirect(offsets[:]), proj[t][:], ADD)
+        for c, cols in enumerate(chunks):
+            nc.scalar.activation(hidden[c][:, :, 0:2], early[:, :, cols].rearrange("p t n -> p n t"), GELU)
+
+        late = [sb.tile([P, 2, w], F32, name=f"late{c}", align_bytes=64) for c, w in enumerate(WIDTHS)]
+        for t in range(2, PACK):
+            for c, cols in enumerate(chunks):
+                picks = offsets[:, cols.start // 16 : cols.stop // 16]
+                nc.vector.tensor_tensor(late[c][:, t - 2, :], pe_table[t][:].indirect(picks), proj[t][:, cols], ADD)
+
+        for c in range(len(chunks)):
+            nc.scalar.activation(hidden[c][:, :, 2:4], late[c][:].rearrange("p t n -> p n t"), GELU)
+        result = []
+        for c, w in enumerate(WIDTHS):
+            h_codes = sb.tile([P, w], U32, name=f"h_codes{c}", align_bytes=64)
+            h_scales = sb.tile([P, w], U8, name=f"h_scales{c}", align_bytes=64)
+            nc.vector.quantize_mx(h_codes[:].bitcast(FP8X4), h_scales[:], hidden[c][:].rearrange("p n t -> p (n t)"))
+            res = ps.tile([P, w], F32, name=f"res{c}", tag=f"bank{(PACK + c) % 8}")
+            nc.tensor.matmul_mx(
+                res[:],
+                lhsT=w2_codes[:].bitcast(FP8X4),
+                lhsT_scale=w2_scales[:],
+                rhs=h_codes[:].bitcast(FP8X4),
+                rhs_scale=h_scales[:],
+                start=True,
+                stop=True,
+            )
+            result.append(res)
+        for c, cols in enumerate(chunks):
+            staged = sb.tile([P, WIDTHS[c]], F32, name=f"staged{c}", align_bytes=64)
+            nc.scalar.copy(staged[:], result[c][:])
+            nc.sync.dma_start(out[:, cols], staged[:])

@@ -37,16 +37,22 @@ def tile_picked_posadd_gelu_p_kernel(tc, x_words, x_scales, w1, w2, pe, offs, ou
         nc.vector.memset(scale_table[:].bitcast(I32), 0)
         scale_rows = x_scales.rearrange("z (q r) c -> r q z c", r=4)
 
-        w1_raw = [sb.tile([P, PACK, H], F32, name=f"w1_raw{z}", tag=("w1_first", "slot2")[z], align_bytes=64) for z in range(PASSES)]
-        word_table = [sb.tile([P, T], U16, name=f"word_table{z}", tag=f"slot{2 * z + 1}", align_bytes=64) for z in range(PASSES)]
-        nc.sync.dma_start(w1_raw[0][:], w1[0:K_PASS, :].rearrange("(p j) c -> p j c", j=PACK))
+        warm_in = sb.tile([P, 1], F32, name="warm_in")
+        warm_out = sb.tile([P, 1], F32, name="warm_out")
+        nc.gpsimd.memset(warm_in[:], 0.0)
+        nc.scalar.activation(warm_out[:], warm_in[:], GELU)
+
+        w1_raw = [sb.tile([P, PACK, H], F32, name=f"w1_raw{z}", tag=("slot_w2", "slot2")[z], align_bytes=64) for z in range(PASSES)]
+        word_table = [sb.tile([P, T], U16, name=f"word_table{z}", tag=("words0", "slot3")[z], align_bytes=64) for z in range(PASSES)]
+        nc.sync.dma_start(word_table[0][:].bitcast(I32), x_words[0].bitcast(I32))
         for r in range(4):
             nc.sync.dma_start(scale_table[r:P:16, :].bitcast(I32), scale_rows[r].bitcast(I32))
-        nc.sync.dma_start(word_table[0][:].bitcast(I32), x_words[0].bitcast(I32))
+        nc.sync.dma_start(w1_raw[0][:], w1[0:K_PASS, :].rearrange("(p j) c -> p j c", j=PACK))
         nc.sync.dma_start(w1_raw[1][:], w1[K_PASS:K, :].rearrange("(p j) c -> p j c", j=PACK))
         nc.sync.dma_start(word_table[1][:].bitcast(I32), x_words[1].bitcast(I32))
-        w2_raw = sb.tile([P, PACK, N], F32, name="w2_raw", align_bytes=64)
-        nc.sync.dma_start(w2_raw[:], w2.rearrange("(p j) c -> p j c", j=PACK))
+
+        x_code = [sb.tile([P, S], U16, name=f"x_code{z}", align_bytes=64) for z in range(PASSES)]
+        nc.vector.tensor_copy(x_code[0][:], word_table[0][:].indirect(offsets[:]))
 
         x_scale = [sb.tile([P, S], U8, name=f"x_scale{z}", align_bytes=64) for z in range(PASSES)]
         nc.vector.memset(x_scale[1][96:P, :].bitcast(I32), 0)
@@ -55,38 +61,43 @@ def tile_picked_posadd_gelu_p_kernel(tc, x_words, x_scales, w1, w2, pe, offs, ou
         pe_rows = pe.rearrange("(p t) c -> t p c", t=PACK)
         pe_table = []
 
+        def load_pe(t):
+            pe_table.append(sb.tile([P, T], F32, name=f"pe_table{t}", tag=f"slot{t}", align_bytes=64))
+            nc.sync.dma_start(pe_table[t][:], pe_rows[t])
+
+        load_pe(0)
         acc = [ps.tile([P, S], F32, name=f"acc{t}", tag=f"bank{t}") for t in range(PACK)]
         for z in range(PASSES):
-            grouped = [sb.tile([P, 2, P, PACK], BF16, name=f"w1_grouped{z}{u}", align_bytes=64) for u in range(2)]
+            grouped = [
+                sb.tile([P, 2, P, PACK], BF16, name=f"w1_grouped{z}{u}", tag=("slot1" if z + u == 0 else f"grouped{z}{u}"), align_bytes=64)
+                for u in range(2)
+            ]
             src = w1_raw[z][:].rearrange("p j (m t) -> p m t j", t=PACK)
             nc.vector.tensor_copy(grouped[0][:].rearrange("p t m j -> p m t j"), src[:, :, 0:2, :])
             nc.scalar.copy(grouped[1][:].rearrange("p t m j -> p m t j"), src[:, :, 2:4, :])
-            x_code = sb.tile([P, S], U16, name=f"x_code{z}", align_bytes=64)
-            nc.vector.tensor_copy(x_code[:], word_table[z][:].indirect(offsets[:]))
-            for t in (2 * z, 2 * z + 1):
-                pe_table.append(sb.tile([P, T], F32, name=f"pe_table{t}", tag=f"slot{t}", align_bytes=64))
-                nc.sync.dma_start(pe_table[t][:], pe_rows[t])
             for u in range(2):
                 codes = sb.tile([P, 2 * P], U32, name=f"w1_codes{z}{u}", align_bytes=64)
                 scales = sb.tile([P, 2 * P], U8, name=f"w1_scales{z}{u}", align_bytes=64)
                 nc.vector.quantize_mx(codes[:].bitcast(FP8X4), scales[:], grouped[u][:].rearrange("p t m j -> p (t m j)"))
+                if z == 1 and u == 0:
+                    nc.vector.tensor_copy(x_code[1][:], word_table[1][:].indirect(offsets[:]))
                 for v in range(2):
                     cols = slice(v * P, (v + 1) * P)
                     nc.tensor.matmul_mx(
                         acc[2 * u + v][:],
                         lhsT=codes[:, cols].bitcast(FP8X4),
                         lhsT_scale=scales[:, cols],
-                        rhs=x_code[:].bitcast(FP4X4),
+                        rhs=x_code[z][:].bitcast(FP4X4),
                         rhs_scale=x_scale[z][:],
                         start=(z == 0),
                         stop=(z == PASSES - 1),
                     )
-
-        w2_grouped = sb.tile([P, N, PACK], BF16, name="w2_grouped", align_bytes=64)
-        nc.vector.tensor_copy(w2_grouped[:], w2_raw[:].rearrange("p j c -> p c j"))
-        w2_codes = sb.tile([P, N], U32, name="w2_codes", align_bytes=64)
-        w2_scales = sb.tile([P, N], U8, name="w2_scales", align_bytes=64)
-        nc.vector.quantize_mx(w2_codes[:].bitcast(FP8X4), w2_scales[:], w2_grouped[:].rearrange("p c j -> p (c j)"))
+            if z == 0:
+                load_pe(1)
+                w2_raw = sb.tile([P, PACK, N], F32, name="w2_raw", tag="slot_w2", align_bytes=64)
+                nc.sync.dma_start(w2_raw[:], w2.rearrange("(p j) c -> p j c", j=PACK))
+        load_pe(2)
+        load_pe(3)
 
         proj = [sb.tile([P, S], F32, name=f"proj{t}", align_bytes=64) for t in range(PACK)]
         for t in range(PACK):
@@ -99,6 +110,12 @@ def tile_picked_posadd_gelu_p_kernel(tc, x_words, x_scales, w1, w2, pe, offs, ou
             nc.vector.tensor_tensor(early[:, t, :], pe_table[t][:].indirect(offsets[:]), proj[t][:], ADD)
         for c, cols in enumerate(chunks):
             nc.scalar.activation(hidden[c][:, :, 0:2], early[:, :, cols].rearrange("p t n -> p n t"), GELU)
+
+        w2_grouped = sb.tile([P, N, PACK], BF16, name="w2_grouped", align_bytes=64)
+        nc.vector.tensor_copy(w2_grouped[:], w2_raw[:].rearrange("p j c -> p c j"))
+        w2_codes = sb.tile([P, N], U32, name="w2_codes", align_bytes=64)
+        w2_scales = sb.tile([P, N], U8, name="w2_scales", align_bytes=64)
+        nc.vector.quantize_mx(w2_codes[:].bitcast(FP8X4), w2_scales[:], w2_grouped[:].rearrange("p c j -> p (c j)"))
 
         late = [sb.tile([P, 2, w], F32, name=f"late{c}", align_bytes=64) for c, w in enumerate(WIDTHS)]
         for t in range(2, PACK):
@@ -126,5 +143,8 @@ def tile_picked_posadd_gelu_p_kernel(tc, x_words, x_scales, w1, w2, pe, offs, ou
             result.append(res)
         for c, cols in enumerate(chunks):
             staged = sb.tile([P, WIDTHS[c]], F32, name=f"staged{c}", align_bytes=64)
-            nc.scalar.copy(staged[:], result[c][:])
+            if c == len(chunks) - 1:
+                nc.vector.tensor_copy(staged[:], result[c][:])
+            else:
+                nc.scalar.copy(staged[:], result[c][:])
             nc.sync.dma_start(out[:, cols], staged[:])

@@ -31,33 +31,34 @@ def tile_picked_posadd_gelu_p_kernel(tc, x_words, x_scales, w1, w2, pe, offs, ou
         ps = ctx.enter_context(tc.psum_pool(name="ps", bufs=1))
 
         offsets = sb.tile([P, S // 16], U16, name="offsets")
-        nc.sync.dma_start(offsets[:], offs)
 
-        scale_table = sb.tile([P, T], U8, name="scale_table", tag="slot0", align_bytes=64)
-        nc.vector.memset(scale_table[:].bitcast(I32), 0)
-        scale_rows = x_scales.rearrange("z (q r) c -> r q z c", r=4)
+        scale_table = sb.tile([P, T], U8, name="scale_table", tag="slot_x1", align_bytes=64)
+        nc.sync.dma_start(scale_table[0:32, :].bitcast(I32), x_scales.rearrange("z b c -> b z c").bitcast(I32))
+        nc.sync.dma_start(offsets[:], offs)
+        nc.vector.memset(scale_table[32:64, :].bitcast(I32), 0)
+        nc.vector.memset(scale_table[64:P, :].bitcast(I32), 0)
 
         warm_in = sb.tile([P, 1], F32, name="warm_in")
         warm_out = sb.tile([P, 1], F32, name="warm_out")
         nc.gpsimd.memset(warm_in[:], 0.0)
         nc.scalar.activation(warm_out[:], warm_in[:], GELU)
 
-        w1_raw = [sb.tile([P, PACK, H], F32, name=f"w1_raw{z}", tag=("slot_w2", "slot2")[z], align_bytes=64) for z in range(PASSES)]
-        word_table = [sb.tile([P, T], U16, name=f"word_table{z}", tag=("words0", "slot3")[z], align_bytes=64) for z in range(PASSES)]
+        w1_raw = [sb.tile([P, PACK, H], F32, name=f"w1_raw{z}", tag=("slot_w2", "slot3")[z], align_bytes=64) for z in range(PASSES)]
+        word_table = [sb.tile([P, T], U16, name="word_table0", tag="slot0", align_bytes=64)]
         nc.sync.dma_start(word_table[0][:].bitcast(I32), x_words[0].bitcast(I32))
-        for r in range(4):
-            nc.sync.dma_start(scale_table[r:P:16, :].bitcast(I32), scale_rows[r].bitcast(I32))
         nc.sync.dma_start(w1_raw[0][:], w1[0:K_PASS, :].rearrange("(p j) c -> p j c", j=PACK))
         nc.sync.dma_start(w1_raw[1][:], w1[K_PASS:K, :].rearrange("(p j) c -> p j c", j=PACK))
-        nc.sync.dma_start(word_table[1][:].bitcast(I32), x_words[1].bitcast(I32))
 
+        picked_scales = sb.tile([P, S], U8, name="picked_scales", tag="slot2", align_bytes=64)
+        x_scale = sb.tile([P, PASSES * S], U8, name="x_scale", align_bytes=64)
+        nc.vector.memset(x_scale[:].bitcast(I32), 0)
+        nc.vector.tensor_copy(picked_scales[:], scale_table[:].indirect(offsets[:]))
+        for q in range(4):
+            nc.sync.dma_start(x_scale[32 * q : 32 * q + 4, :].bitcast(I32), picked_scales[8 * q : 8 * q + 8, :].bitcast(I32))
+        word_table.append(sb.tile([P, T], U16, name="word_table1", tag="slot_x1", align_bytes=64))
+        nc.sync.dma_start(word_table[1][:].bitcast(I32), x_words[1].bitcast(I32))
         x_code = [sb.tile([P, S], U16, name=f"x_code{z}", align_bytes=64) for z in range(PASSES)]
         nc.vector.tensor_copy(x_code[0][:], word_table[0][:].indirect(offsets[:]))
-
-        x_scale = [sb.tile([P, S], U8, name=f"x_scale{z}", align_bytes=64) for z in range(PASSES)]
-        nc.vector.memset(x_scale[1][96:P, :].bitcast(I32), 0)
-        nc.vector.tensor_copy(x_scale[0][:], scale_table[:].indirect(offsets[:]))
-        nc.sync.dma_start(x_scale[1][0 : P - 16, :].bitcast(I32), x_scale[0][16:P, :].bitcast(I32))
         pe_rows = pe.rearrange("(p t) c -> t p c", t=PACK)
         pe_table = []
 
@@ -88,7 +89,7 @@ def tile_picked_posadd_gelu_p_kernel(tc, x_words, x_scales, w1, w2, pe, offs, ou
                         lhsT=codes[:, cols].bitcast(FP8X4),
                         lhsT_scale=scales[:, cols],
                         rhs=x_code[z][:].bitcast(FP4X4),
-                        rhs_scale=x_scale[z][:],
+                        rhs_scale=x_scale[:, z * S : (z + 1) * S],
                         start=(z == 0),
                         stop=(z == PASSES - 1),
                     )
@@ -145,6 +146,7 @@ def tile_picked_posadd_gelu_p_kernel(tc, x_words, x_scales, w1, w2, pe, offs, ou
             staged = sb.tile([P, WIDTHS[c]], F32, name=f"staged{c}", align_bytes=64)
             if c == len(chunks) - 1:
                 nc.vector.tensor_copy(staged[:], result[c][:])
+                nc.scalar.dma_start(out[:, cols], staged[:])
             else:
                 nc.scalar.copy(staged[:], result[c][:])
-            nc.sync.dma_start(out[:, cols], staged[:])
+                nc.sync.dma_start(out[:, cols], staged[:])

@@ -38,23 +38,18 @@ def tile_picked_posadd_gelu_p_kernel(tc, x_words, x_scales, w1, w2, pe, offs, ou
         nc.vector.memset(scale_table[32:64, :].bitcast(I32), 0)
         nc.vector.memset(scale_table[64:P, :].bitcast(I32), 0)
 
-        warm_in = sb.tile([P, 1], F32, name="warm_in")
-        warm_out = sb.tile([P, 1], F32, name="warm_out")
-        nc.gpsimd.memset(warm_in[:], 0.0)
-        nc.scalar.activation(warm_out[:], warm_in[:], GELU)
-
-        w1_raw = [sb.tile([P, PACK, H], F32, name=f"w1_raw{z}", tag=("slot_w2", "slot3")[z], align_bytes=64) for z in range(PASSES)]
+        w1_raw = [sb.tile([P, PACK, H], F32, name=f"w1_raw{z}", tag=("slot2", "slot_w2")[z], align_bytes=64) for z in range(PASSES)]
         word_table = [sb.tile([P, T], U16, name="word_table0", tag="slot0", align_bytes=64)]
         nc.sync.dma_start(word_table[0][:].bitcast(I32), x_words[0].bitcast(I32))
         nc.sync.dma_start(w1_raw[0][:], w1[0:K_PASS, :].rearrange("(p j) c -> p j c", j=PACK))
         nc.sync.dma_start(w1_raw[1][:], w1[K_PASS:K, :].rearrange("(p j) c -> p j c", j=PACK))
 
-        picked_scales = sb.tile([P, S], U8, name="picked_scales", tag="slot2", align_bytes=64)
+        picked_scales = sb.tile([P, S], U8, name="picked_scales", tag="slot3", align_bytes=64)
         x_scale = sb.tile([P, PASSES * S], U8, name="x_scale", align_bytes=64)
         nc.vector.memset(x_scale[:].bitcast(I32), 0)
         nc.vector.tensor_copy(picked_scales[:], scale_table[:].indirect(offsets[:]))
         for q in range(4):
-            nc.sync.dma_start(x_scale[32 * q : 32 * q + 4, :].bitcast(I32), picked_scales[8 * q : 8 * q + 8, :].bitcast(I32))
+            nc.scalar.dma_start(x_scale[32 * q : 32 * q + 4, :].bitcast(I32), picked_scales[8 * q : 8 * q + 8, :].bitcast(I32))
         word_table.append(sb.tile([P, T], U16, name="word_table1", tag="slot_x1", align_bytes=64))
         nc.sync.dma_start(word_table[1][:].bitcast(I32), x_words[1].bitcast(I32))
         x_code = [sb.tile([P, S], U16, name=f"x_code{z}", align_bytes=64) for z in range(PASSES)]
@@ -95,10 +90,10 @@ def tile_picked_posadd_gelu_p_kernel(tc, x_words, x_scales, w1, w2, pe, offs, ou
                     )
             if z == 0:
                 load_pe(1)
-                w2_raw = sb.tile([P, PACK, N], F32, name="w2_raw", tag="slot_w2", align_bytes=64)
-                nc.sync.dma_start(w2_raw[:], w2.rearrange("(p j) c -> p j c", j=PACK))
-        load_pe(2)
-        load_pe(3)
+                load_pe(2)
+                load_pe(3)
+        w2_raw = sb.tile([P, PACK, N], F32, name="w2_raw", tag="slot_w2", align_bytes=64)
+        nc.sync.dma_start(w2_raw[:], w2.rearrange("(p j) c -> p j c", j=PACK))
 
         proj = [sb.tile([P, S], F32, name=f"proj{t}", align_bytes=64) for t in range(PACK)]
         for t in range(PACK):
@@ -112,12 +107,6 @@ def tile_picked_posadd_gelu_p_kernel(tc, x_words, x_scales, w1, w2, pe, offs, ou
         for c, cols in enumerate(chunks):
             nc.scalar.activation(hidden[c][:, :, 0:2], early[:, :, cols].rearrange("p t n -> p n t"), GELU)
 
-        w2_grouped = sb.tile([P, N, PACK], BF16, name="w2_grouped", align_bytes=64)
-        nc.vector.tensor_copy(w2_grouped[:], w2_raw[:].rearrange("p j c -> p c j"))
-        w2_codes = sb.tile([P, N], U32, name="w2_codes", align_bytes=64)
-        w2_scales = sb.tile([P, N], U8, name="w2_scales", align_bytes=64)
-        nc.vector.quantize_mx(w2_codes[:].bitcast(FP8X4), w2_scales[:], w2_grouped[:].rearrange("p c j -> p (c j)"))
-
         late = [sb.tile([P, 2, w], F32, name=f"late{c}", align_bytes=64) for c, w in enumerate(WIDTHS)]
         for t in range(2, PACK):
             for c, cols in enumerate(chunks):
@@ -126,6 +115,12 @@ def tile_picked_posadd_gelu_p_kernel(tc, x_words, x_scales, w1, w2, pe, offs, ou
 
         for c in range(len(chunks)):
             nc.scalar.activation(hidden[c][:, :, 2:4], late[c][:].rearrange("p t n -> p n t"), GELU)
+        w2_grouped = sb.tile([P, N, PACK], BF16, name="w2_grouped", align_bytes=64)
+        nc.vector.tensor_copy(w2_grouped[:], w2_raw[:].rearrange("p j c -> p c j"))
+        w2_codes = sb.tile([P, N], U32, name="w2_codes", align_bytes=64)
+        w2_scales = sb.tile([P, N], U8, name="w2_scales", align_bytes=64)
+        nc.vector.quantize_mx(w2_codes[:].bitcast(FP8X4), w2_scales[:], w2_grouped[:].rearrange("p c j -> p (c j)"))
+
         result = []
         for c, w in enumerate(WIDTHS):
             h_codes = sb.tile([P, w], U32, name=f"h_codes{c}", align_bytes=64)

@@ -115,7 +115,7 @@ def tile_picked_posadd_gelu_p_kernel(tc, x_words, x_scales, w1, w2, pe, offs, ou
 
         for c in range(len(chunks)):
             nc.scalar.activation(hidden[c][:, :, 2:4], late[c][:].rearrange("p t n -> p n t"), GELU)
-        w2_grouped = sb.tile([P, N, PACK], BF16, name="w2_grouped", align_bytes=64)
+        w2_grouped = sb.tile([P, N, PACK], BF16, name="w2_grouped", tag="w2_grouped", align_bytes=64)
         nc.vector.tensor_copy(w2_grouped[:], w2_raw[:].rearrange("p j c -> p c j"))
         w2_codes = sb.tile([P, N], U32, name="w2_codes", align_bytes=64)
         w2_scales = sb.tile([P, N], U8, name="w2_scales", align_bytes=64)
@@ -123,7 +123,8 @@ def tile_picked_posadd_gelu_p_kernel(tc, x_words, x_scales, w1, w2, pe, offs, ou
 
         result = []
         for c, w in enumerate(WIDTHS):
-            h_codes = sb.tile([P, w], U32, name=f"h_codes{c}", align_bytes=64)
+            code_tag = {len(WIDTHS) - 2: "slot_w2", len(WIDTHS) - 1: "w2_grouped"}.get(c, f"h_codes{c}")
+            h_codes = sb.tile([P, w], U32, name=f"h_codes{c}", tag=code_tag, align_bytes=64)
             h_scales = sb.tile([P, w], U8, name=f"h_scales{c}", align_bytes=64)
             nc.vector.quantize_mx(h_codes[:].bitcast(FP8X4), h_scales[:], hidden[c][:].rearrange("p n t -> p (n t)"))
             res = ps.tile([P, w], F32, name=f"res{c}", tag=f"bank{(PACK + c) % 8}")

@@ -32,15 +32,16 @@ def tile_picked_posadd_gelu_p_kernel(tc, x_words, x_scales, w1, w2, pe, offs, ou
 
         offsets = sb.tile([P, S // 16], U16, name="offsets")
 
-        scale_table = sb.tile([P, T], U8, name="scale_table", tag="slot_x1", align_bytes=64)
-        nc.sync.dma_start(scale_table[0:32, :].bitcast(I32), x_scales.rearrange("z b c -> b z c").bitcast(I32))
+        scale_table = sb.tile([P, T], U8, name="scale_table", tag="slot1", align_bytes=64)
+        nc.scalar.dma_start(scale_table[0:32, :].bitcast(I32), x_scales.rearrange("z b c -> b z c").bitcast(I32))
         nc.sync.dma_start(offsets[:], offs)
         nc.vector.memset(scale_table[32:64, :].bitcast(I32), 0)
         nc.vector.memset(scale_table[64:P, :].bitcast(I32), 0)
 
         w1_raw = [sb.tile([P, PACK, H], F32, name=f"w1_raw{z}", tag=("slot2", "slot_w2")[z], align_bytes=64) for z in range(PASSES)]
-        word_table = [sb.tile([P, T], U16, name="word_table0", tag="slot0", align_bytes=64)]
-        nc.sync.dma_start(word_table[0][:].bitcast(I32), x_words[0].bitcast(I32))
+        word_table = [sb.tile([P, T], U16, name=f"word_table{z}", align_bytes=64) for z in range(PASSES)]
+        for z in range(PASSES):
+            nc.scalar.dma_start(word_table[z][:].bitcast(I32), x_words[z].bitcast(I32))
         nc.sync.dma_start(w1_raw[0][:], w1[0:K_PASS, :].rearrange("(p j) c -> p j c", j=PACK))
         nc.sync.dma_start(w1_raw[1][:], w1[K_PASS:K, :].rearrange("(p j) c -> p j c", j=PACK))
 
@@ -50,8 +51,6 @@ def tile_picked_posadd_gelu_p_kernel(tc, x_words, x_scales, w1, w2, pe, offs, ou
         nc.vector.tensor_copy(picked_scales[:], scale_table[:].indirect(offsets[:]))
         for q in range(4):
             nc.scalar.dma_start(x_scale[32 * q : 32 * q + 4, :].bitcast(I32), picked_scales[8 * q : 8 * q + 8, :].bitcast(I32))
-        word_table.append(sb.tile([P, T], U16, name="word_table1", tag="slot_x1", align_bytes=64))
-        nc.sync.dma_start(word_table[1][:].bitcast(I32), x_words[1].bitcast(I32))
         x_code = [sb.tile([P, S], U16, name=f"x_code{z}", align_bytes=64) for z in range(PASSES)]
         nc.vector.tensor_copy(x_code[0][:], word_table[0][:].indirect(offsets[:]))
         pe_rows = pe.rearrange("(p t) c -> t p c", t=PACK)
@@ -65,7 +64,7 @@ def tile_picked_posadd_gelu_p_kernel(tc, x_words, x_scales, w1, w2, pe, offs, ou
         acc = [ps.tile([P, S], F32, name=f"acc{t}", tag=f"bank{t}") for t in range(PACK)]
         for z in range(PASSES):
             grouped = [
-                sb.tile([P, 2, P, PACK], BF16, name=f"w1_grouped{z}{u}", tag=("slot1" if z + u == 0 else f"grouped{z}{u}"), align_bytes=64)
+                sb.tile([P, 2, P, PACK], BF16, name=f"w1_grouped{z}{u}", align_bytes=64)
                 for u in range(2)
             ]
             src = w1_raw[z][:].rearrange("p j (m t) -> p m t j", t=PACK)

@@ -34,16 +34,16 @@ def tile_picked_posadd_gelu_p_kernel(tc, x_words, x_scales, w1, w2, pe, offs, ou
 
         scale_table = sb.tile([P, T], U8, name="scale_table", tag="slot1", align_bytes=64)
         nc.scalar.dma_start(scale_table[0:32, :].bitcast(I32), x_scales.rearrange("z b c -> b z c").bitcast(I32))
-        nc.sync.dma_start(offsets[:], offs)
         nc.vector.memset(scale_table[32:64, :].bitcast(I32), 0)
         nc.vector.memset(scale_table[64:P, :].bitcast(I32), 0)
 
         w1_raw = [sb.tile([P, PACK, H], F32, name=f"w1_raw{z}", tag=("slot2", "slot_w2")[z], align_bytes=64) for z in range(PASSES)]
         word_table = [sb.tile([P, T], U16, name=f"word_table{z}", align_bytes=64) for z in range(PASSES)]
-        for z in range(PASSES):
-            nc.scalar.dma_start(word_table[z][:].bitcast(I32), x_words[z].bitcast(I32))
+        nc.sync.dma_start(word_table[0][:].bitcast(I32), x_words[0].bitcast(I32))
+        nc.sync.dma_start(offsets[:], offs)
         nc.sync.dma_start(w1_raw[0][:], w1[0:K_PASS, :].rearrange("(p j) c -> p j c", j=PACK))
         nc.sync.dma_start(w1_raw[1][:], w1[K_PASS:K, :].rearrange("(p j) c -> p j c", j=PACK))
+        nc.sync.dma_start(word_table[1][:].bitcast(I32), x_words[1].bitcast(I32))
 
         picked_scales = sb.tile([P, S], U8, name="picked_scales", tag="slot3", align_bytes=64)
         x_scale = sb.tile([P, PASSES * S], U8, name="x_scale", align_bytes=64)

@@ -38,7 +38,7 @@ def tile_picked_posadd_gelu_p_kernel(tc, x_words, x_scales, w1, w2, pe, offs, ou
         nc.vector.memset(scale_table[64:P, :].bitcast(I32), 0)
 
         w1_raw = [sb.tile([P, PACK, H], F32, name=f"w1_raw{z}", tag=("slot2", "slot_w2")[z], align_bytes=64) for z in range(PASSES)]
-        word_table = [sb.tile([P, T], U16, name=f"word_table{z}", align_bytes=64) for z in range(PASSES)]
+        word_table = [sb.tile([P, T], U16, name=f"word_table{z}", tag=("slot0", "words1")[z], align_bytes=64) for z in range(PASSES)]
         nc.sync.dma_start(word_table[0][:].bitcast(I32), x_words[0].bitcast(I32))
         nc.sync.dma_start(offsets[:], offs)
         nc.sync.dma_start(w1_raw[0][:], w1[0:K_PASS, :].rearrange("(p j) c -> p j c", j=PACK))

@@ -115,24 +115,33 @@ def tile_picked_posadd_gelu_p_kernel(tc, x_words, x_scales, w1, w2, pe, offs, ou
         for c in range(len(chunks)):
             nc.scalar.activation(hidden[c][:, :, 2:4], late[c][:].rearrange("p t n -> p n t"), GELU)
         w2_grouped = sb.tile([P, N, PACK], BF16, name="w2_grouped", tag="w2_grouped", align_bytes=64)
-        nc.vector.tensor_copy(w2_grouped[:], w2_raw[:].rearrange("p j c -> p c j"))
+        nc.vector.tensor_copy(
+            w2_grouped[:].rearrange("p (c i) j -> p c j i", i=PACK),
+            w2_raw[:].rearrange("p j (c i) -> p c j i", i=PACK),
+        )
         w2_codes = sb.tile([P, N], U32, name="w2_codes", align_bytes=64)
         w2_scales = sb.tile([P, N], U8, name="w2_scales", align_bytes=64)
+        h_codes = [sb.tile([P, w], U32, name=f"h_codes{c}", align_bytes=64) for c, w in enumerate(WIDTHS)]
+        h_scales = [sb.tile([P, w], U8, name=f"h_scales{c}", align_bytes=64) for c, w in enumerate(WIDTHS)]
+
+        def quantise_h(c):
+            nc.vector.quantize_mx(h_codes[c][:].bitcast(FP8X4), h_scales[c][:], hidden[c][:].rearrange("p n t -> p (n t)"))
+
+        quantise_h(0)
+        quantise_h(1)
         nc.vector.quantize_mx(w2_codes[:].bitcast(FP8X4), w2_scales[:], w2_grouped[:].rearrange("p c j -> p (c j)"))
+        for c in range(2, len(WIDTHS)):
+            quantise_h(c)
 
         result = []
         for c, w in enumerate(WIDTHS):
-            code_tag = {len(WIDTHS) - 2: "slot_w2", len(WIDTHS) - 1: "w2_grouped"}.get(c, f"h_codes{c}")
-            h_codes = sb.tile([P, w], U32, name=f"h_codes{c}", tag=code_tag, align_bytes=64)
-            h_scales = sb.tile([P, w], U8, name=f"h_scales{c}", align_bytes=64)
-            nc.vector.quantize_mx(h_codes[:].bitcast(FP8X4), h_scales[:], hidden[c][:].rearrange("p n t -> p (n t)"))
             res = ps.tile([P, w], F32, name=f"res{c}", tag=f"bank{(PACK + c) % 8}")
             nc.tensor.matmul_mx(
                 res[:],
                 lhsT=w2_codes[:].bitcast(FP8X4),
                 lhsT_scale=w2_scales[:],
-                rhs=h_codes[:].bitcast(FP8X4),
-                rhs_scale=h_scales[:],
+                rhs=h_codes[c][:].bitcast(FP8X4),
+                rhs_scale=h_scales[c][:],
                 start=True,
                 stop=True,
             )
@@ -141,7 +150,7 @@ def tile_picked_posadd_gelu_p_kernel(tc, x_words, x_scales, w1, w2, pe, offs, ou
             staged = sb.tile([P, WIDTHS[c]], F32, name=f"staged{c}", align_bytes=64)
             if c == len(chunks) - 1:
                 nc.vector.tensor_copy(staged[:], result[c][:])
-                nc.scalar.dma_start(out[:, cols], staged[:])
             else:
                 nc.scalar.copy(staged[:], result[c][:])
-                nc.sync.dma_start(out[:, cols], staged[:])
+            queue = nc.scalar if c == len(chunks) - 2 else nc.sync
+            queue.dma_start(out[:, cols], staged[:])

@@ -39,8 +39,8 @@ def tile_picked_posadd_gelu_p_kernel(tc, x_words, x_scales, w1, w2, pe, offs, ou
 
         w1_raw = [sb.tile([P, PACK, H], F32, name=f"w1_raw{z}", tag=("slot2", "slot_w2")[z], align_bytes=64) for z in range(PASSES)]
         word_table = [sb.tile([P, T], U16, name=f"word_table{z}", tag=("slot0", "words1")[z], align_bytes=64) for z in range(PASSES)]
-        nc.sync.dma_start(word_table[0][:].bitcast(I32), x_words[0].bitcast(I32))
         nc.sync.dma_start(offsets[:], offs)
+        nc.sync.dma_start(word_table[0][:].bitcast(I32), x_words[0].bitcast(I32))
         nc.sync.dma_start(w1_raw[0][:], w1[0:K_PASS, :].rearrange("(p j) c -> p j c", j=PACK))
         nc.sync.dma_start(w1_raw[1][:], w1[K_PASS:K, :].rearrange("(p j) c -> p j c", j=PACK))
         nc.sync.dma_start(word_table[1][:].bitcast(I32), x_words[1].bitcast(I32))
@@ -61,36 +61,43 @@ def tile_picked_posadd_gelu_p_kernel(tc, x_words, x_scales, w1, w2, pe, offs, ou
             nc.sync.dma_start(pe_table[t][:], pe_rows[t])
 
         load_pe(0)
+        warm = sb.tile([P, 1], F32, name="warm", align_bytes=64)
+        nc.scalar.activation(warm[:], w1_raw[0][:, 0, 0:1], GELU)
         acc = [ps.tile([P, S], F32, name=f"acc{t}", tag=f"bank{t}") for t in range(PACK)]
+        grouped = {}
         for z in range(PASSES):
-            grouped = [
-                sb.tile([P, 2, P, PACK], BF16, name=f"w1_grouped{z}{u}", align_bytes=64)
-                for u in range(2)
-            ]
             src = w1_raw[z][:].rearrange("p j (m t) -> p m t j", t=PACK)
-            nc.vector.tensor_copy(grouped[0][:].rearrange("p t m j -> p m t j"), src[:, :, 0:2, :])
-            nc.scalar.copy(grouped[1][:].rearrange("p t m j -> p m t j"), src[:, :, 2:4, :])
             for u in range(2):
-                codes = sb.tile([P, 2 * P], U32, name=f"w1_codes{z}{u}", align_bytes=64)
-                scales = sb.tile([P, 2 * P], U8, name=f"w1_scales{z}{u}", align_bytes=64)
-                nc.vector.quantize_mx(codes[:].bitcast(FP8X4), scales[:], grouped[u][:].rearrange("p t m j -> p (t m j)"))
-                if z == 1 and u == 0:
-                    nc.vector.tensor_copy(x_code[1][:], word_table[1][:].indirect(offsets[:]))
-                for v in range(2):
-                    cols = slice(v * P, (v + 1) * P)
-                    nc.tensor.matmul_mx(
-                        acc[2 * u + v][:],
-                        lhsT=codes[:, cols].bitcast(FP8X4),
-                        lhsT_scale=scales[:, cols],
-                        rhs=x_code[z][:].bitcast(FP4X4),
-                        rhs_scale=x_scale[:, z * S : (z + 1) * S],
-                        start=(z == 0),
-                        stop=(z == PASSES - 1),
-                    )
+                grouped[z, u] = sb.tile([P, 2, P, PACK], BF16, name=f"w1_grouped{z}{u}", align_bytes=64)
+            nc.vector.tensor_copy(grouped[z, 0][:].rearrange("p t m j -> p m t j"), src[:, :, 0:2, :])
+            nc.scalar.copy(grouped[z, 1][:].rearrange("p t m j -> p m t j"), src[:, :, 2:4, :])
             if z == 0:
                 load_pe(1)
                 load_pe(2)
                 load_pe(3)
+        w1_mx = {}
+        for u in range(2):
+            for z in range(PASSES):
+                tag = "words1" if (z, u) == (0, 1) else f"w1_codes{z}{u}"
+                codes = sb.tile([P, 2 * P], U32, name=f"w1_codes{z}{u}", tag=tag, align_bytes=64)
+                scales = sb.tile([P, 2 * P], U8, name=f"w1_scales{z}{u}", align_bytes=64)
+                nc.vector.quantize_mx(codes[:].bitcast(FP8X4), scales[:], grouped[z, u][:].rearrange("p t m j -> p (t m j)"))
+                w1_mx[z, u] = (codes, scales)
+            if u == 0:
+                nc.vector.tensor_copy(x_code[1][:], word_table[1][:].indirect(offsets[:]))
+        for t in range(PACK):
+            for z in range(PASSES):
+                codes, scales = w1_mx[z, t // 2]
+                cols = slice(t % 2 * P, (t % 2 + 1) * P)
+                nc.tensor.matmul_mx(
+                    acc[t][:],
+                    lhsT=codes[:, cols].bitcast(FP8X4),
+                    lhsT_scale=scales[:, cols],
+                    rhs=x_code[z][:].bitcast(FP4X4),
+                    rhs_scale=x_scale[:, z * S : (z + 1) * S],
+                    start=(z == 0),
+                    stop=(z == PASSES - 1),
+                )
         w2_raw = sb.tile([P, PACK, N], F32, name="w2_raw", tag="slot_w2", align_bytes=64)
         nc.sync.dma_start(w2_raw[:], w2.rearrange("(p j) c -> p j c", j=PACK))
 
@@ -100,11 +107,20 @@ def tile_picked_posadd_gelu_p_kernel(tc, x_words, x_scales, w1, w2, pe, offs, ou
 
         chunks = [slice(a, a + w) for a, w in zip(STARTS, WIDTHS)]
         hidden = [sb.tile([P, w, PACK], BF16, name=f"hidden{c}", align_bytes=64) for c, w in enumerate(WIDTHS)]
-        early = sb.tile([P, 2, S], F32, name="early", align_bytes=64)
+        spans = (range(0, 2), range(2, len(WIDTHS)))
+        early = []
+        for g, span in enumerate(spans):
+            width = chunks[span.stop - 1].stop - chunks[span.start].start
+            early.append(sb.tile([P, 2, width], F32, name=f"early{g}", align_bytes=64))
         for t in range(2):
-            nc.vector.tensor_tensor(early[:, t, :], pe_table[t][:].indirect(offsets[:]), proj[t][:], ADD)
-        for c, cols in enumerate(chunks):
-            nc.scalar.activation(hidden[c][:, :, 0:2], early[:, :, cols].rearrange("p t n -> p n t"), GELU)
+            for g, span in enumerate(spans):
+                a, b = chunks[span.start].start, chunks[span.stop - 1].stop
+                nc.vector.tensor_tensor(early[g][:, t, :], pe_table[t][:].indirect(offsets[:, a // 16 : b // 16]), proj[t][:, a:b], ADD)
+        for g, span in enumerate(spans):
+            a = chunks[span.start].start
+            for c in span:
+                part = early[g][:, :, chunks[c].start - a : chunks[c].stop - a]
+                nc.scalar.activation(hidden[c][:, :, 0:2], part.rearrange("p t n -> p n t"), GELU)
 
         late = [sb.tile([P, 2, w], F32, name=f"late{c}", align_bytes=64) for c, w in enumerate(WIDTHS)]
         for t in range(2, PACK):

@@ -33,14 +33,14 @@ def tile_picked_posadd_gelu_p_kernel(tc, x_words, x_scales, w1, w2, pe, offs, ou
         offsets = sb.tile([P, S // 16], U16, name="offsets")
 
         scale_table = sb.tile([P, T], U8, name="scale_table", tag="slot1", align_bytes=64)
-        nc.scalar.dma_start(scale_table[0:32, :].bitcast(I32), x_scales.rearrange("z b c -> b z c").bitcast(I32))
-        nc.vector.memset(scale_table[32:64, :].bitcast(I32), 0)
-        nc.vector.memset(scale_table[64:P, :].bitcast(I32), 0)
+        nc.scalar.dma_start(scale_table[64:96, :].bitcast(I32), x_scales.rearrange("z b c -> b z c").bitcast(I32))
+        nc.vector.memset(scale_table[0:64, :].bitcast(I32), 0)
+        nc.vector.memset(scale_table[96:P, :].bitcast(I32), 0)
 
         w1_raw = [sb.tile([P, PACK, H], F32, name=f"w1_raw{z}", tag=("slot2", "slot_w2")[z], align_bytes=64) for z in range(PASSES)]
         word_table = [sb.tile([P, T], U16, name=f"word_table{z}", tag=("slot0", "words1")[z], align_bytes=64) for z in range(PASSES)]
-        nc.sync.dma_start(offsets[:], offs)
         nc.sync.dma_start(word_table[0][:].bitcast(I32), x_words[0].bitcast(I32))
+        nc.sync.dma_start(offsets[:], offs)
         nc.sync.dma_start(w1_raw[0][:], w1[0:K_PASS, :].rearrange("(p j) c -> p j c", j=PACK))
         nc.sync.dma_start(w1_raw[1][:], w1[K_PASS:K, :].rearrange("(p j) c -> p j c", j=PACK))
         nc.sync.dma_start(word_table[1][:].bitcast(I32), x_words[1].bitcast(I32))
@@ -50,7 +50,7 @@ def tile_picked_posadd_gelu_p_kernel(tc, x_words, x_scales, w1, w2, pe, offs, ou
         nc.vector.memset(x_scale[:].bitcast(I32), 0)
         nc.vector.tensor_copy(picked_scales[:], scale_table[:].indirect(offsets[:]))
         for q in range(4):
-            nc.scalar.dma_start(x_scale[32 * q : 32 * q + 4, :].bitcast(I32), picked_scales[8 * q : 8 * q + 8, :].bitcast(I32))
+            nc.scalar.dma_start(x_scale[32 * q : 32 * q + 4, :].bitcast(I32), picked_scales[64 + 8 * q : 64 + 8 * q + 8, :].bitcast(I32))
         x_code = [sb.tile([P, S], U16, name=f"x_code{z}", align_bytes=64) for z in range(PASSES)]
         nc.vector.tensor_copy(x_code[0][:], word_table[0][:].indirect(offsets[:]))
         pe_rows = pe.rearrange("(p t) c -> t p c", t=PACK)
@@ -61,8 +61,6 @@ def tile_picked_posadd_gelu_p_kernel(tc, x_words, x_scales, w1, w2, pe, offs, ou
             nc.sync.dma_start(pe_table[t][:], pe_rows[t])
 
         load_pe(0)
-        warm = sb.tile([P, 1], F32, name="warm", align_bytes=64)
-        nc.scalar.activation(warm[:], w1_raw[0][:, 0, 0:1], GELU)
         acc = [ps.tile([P, S], F32, name=f"acc{t}", tag=f"bank{t}") for t in range(PACK)]
         grouped = {}
         for z in range(PASSES):
@@ -122,14 +120,20 @@ def tile_picked_posadd_gelu_p_kernel(tc, x_words, x_scales, w1, w2, pe, offs, ou
                 part = early[g][:, :, chunks[c].start - a : chunks[c].stop - a]
                 nc.scalar.activation(hidden[c][:, :, 0:2], part.rearrange("p t n -> p n t"), GELU)
 
-        late = [sb.tile([P, 2, w], F32, name=f"late{c}", align_bytes=64) for c, w in enumerate(WIDTHS)]
+        late_spans = (range(0, 1), range(1, 2), range(2, 3), range(3, 5))
+        late = []
+        for g, span in enumerate(late_spans):
+            width = chunks[span.stop - 1].stop - chunks[span.start].start
+            late.append(sb.tile([P, 2, width], F32, name=f"late{g}", align_bytes=64))
         for t in range(2, PACK):
-            for c, cols in enumerate(chunks):
-                picks = offsets[:, cols.start // 16 : cols.stop // 16]
-                nc.vector.tensor_tensor(late[c][:, t - 2, :], pe_table[t][:].indirect(picks), proj[t][:, cols], ADD)
-
-        for c in range(len(chunks)):
-            nc.scalar.activation(hidden[c][:, :, 2:4], late[c][:].rearrange("p t n -> p n t"), GELU)
+            for g, span in enumerate(late_spans):
+                a, b = chunks[span.start].start, chunks[span.stop - 1].stop
+                nc.vector.tensor_tensor(late[g][:, t - 2, :], pe_table[t][:].indirect(offsets[:, a // 16 : b // 16]), proj[t][:, a:b], ADD)
+        for g, span in enumerate(late_spans):
+            a = chunks[span.start].start
+            for c in span:
+                part = late[g][:, :, chunks[c].start - a : chunks[c].stop - a]
+                nc.scalar.activation(hidden[c][:, :, 2:4], part.rearrange("p t n -> p n t"), GELU)
         w2_grouped = sb.tile([P, N, PACK], BF16, name="w2_grouped", tag="w2_grouped", align_bytes=64)
         nc.vector.tensor_copy(
             w2_grouped[:].rearrange("p (c i) j -> p c j i", i=PACK),
@@ -162,11 +166,11 @@ def tile_picked_posadd_gelu_p_kernel(tc, x_words, x_scales, w1, w2, pe, offs, ou
                 stop=True,
             )
             result.append(res)
-        for c, cols in enumerate(chunks):
+        for c in range(3):
             staged = sb.tile([P, WIDTHS[c]], F32, name=f"staged{c}", align_bytes=64)
-            if c == len(chunks) - 1:
-                nc.vector.tensor_copy(staged[:], result[c][:])
-            else:
-                nc.scalar.copy(staged[:], result[c][:])
-            queue = nc.scalar if c == len(chunks) - 2 else nc.sync
-            queue.dma_start(out[:, cols], staged[:])
+            nc.scalar.copy(staged[:], result[c][:])
+            nc.sync.dma_start(out[:, chunks[c]], staged[:])
+        staged = sb.tile([P, WIDTHS[3] + WIDTHS[4]], F32, name="staged3", align_bytes=64)
+        nc.scalar.copy(staged[:, 0 : WIDTHS[3]], result[3][:])
+        nc.vector.tensor_copy(staged[:, WIDTHS[3] :], result[4][:])
+        nc.scalar.dma_start(out[:, STARTS[3] :], staged[:])

@@ -166,11 +166,11 @@ def tile_picked_posadd_gelu_p_kernel(tc, x_words, x_scales, w1, w2, pe, offs, ou
                 stop=True,
             )
             result.append(res)
-        for c in range(3):
+        for c, cols in enumerate(chunks):
             staged = sb.tile([P, WIDTHS[c]], F32, name=f"staged{c}", align_bytes=64)
-            nc.scalar.copy(staged[:], result[c][:])
-            nc.sync.dma_start(out[:, chunks[c]], staged[:])
-        staged = sb.tile([P, WIDTHS[3] + WIDTHS[4]], F32, name="staged3", align_bytes=64)
-        nc.scalar.copy(staged[:, 0 : WIDTHS[3]], result[3][:])
-        nc.vector.tensor_copy(staged[:, WIDTHS[3] :], result[4][:])
-        nc.scalar.dma_start(out[:, STARTS[3] :], staged[:])
+            if c == len(chunks) - 1:
+                nc.vector.tensor_copy(staged[:], result[c][:])
+            else:
+                nc.scalar.copy(staged[:], result[c][:])
+            queue = nc.scalar if c == len(chunks) - 2 else nc.sync
+            queue.dma_start(out[:, cols], staged[:])

@@ -61,6 +61,8 @@ def tile_picked_posadd_gelu_p_kernel(tc, x_words, x_scales, w1, w2, pe, offs, ou
             nc.sync.dma_start(pe_table[t][:], pe_rows[t])
 
         load_pe(0)
+        warm = sb.tile([P, 1], F32, name="warm", align_bytes=64)
+        nc.scalar.activation(warm[:], w1_raw[0][:, 0, 0:1], GELU)
         acc = [ps.tile([P, S], F32, name=f"acc{t}", tag=f"bank{t}") for t in range(PACK)]
         grouped = {}
         for z in range(PASSES):

@@ -54,13 +54,14 @@ def tile_picked_posadd_gelu_p_kernel(tc, x_words, x_scales, w1, w2, pe, offs, ou
         x_code = [sb.tile([P, S], U16, name=f"x_code{z}", align_bytes=64) for z in range(PASSES)]
         nc.vector.tensor_copy(x_code[0][:], word_table[0][:].indirect(offsets[:]))
         pe_rows = pe.rearrange("(p t) c -> t p c", t=PACK)
-        pe_table = []
+        pe_table = {}
 
         def load_pe(t):
-            pe_table.append(sb.tile([P, T], F32, name=f"pe_table{t}", tag=f"slot{t}", align_bytes=64))
+            pe_table[t] = sb.tile([P, T], F32, name=f"pe_table{t}", tag=f"slot{t}", align_bytes=64)
             nc.sync.dma_start(pe_table[t][:], pe_rows[t])
 
-        load_pe(0)
+        pe_pair = sb.tile([P, 2 * T], F32, name="pe_pair", tag="slot0", align_bytes=64)
+        nc.sync.dma_start(pe_pair[:], pe.rearrange("(p t) c -> p (t c)", t=PACK)[:, 0 : 2 * T])
         warm = sb.tile([P, 1], F32, name="warm", align_bytes=64)
         nc.scalar.activation(warm[:], w1_raw[0][:, 0, 0:1], GELU)
         acc = [ps.tile([P, S], F32, name=f"acc{t}", tag=f"bank{t}") for t in range(PACK)]
@@ -72,7 +73,6 @@ def tile_picked_posadd_gelu_p_kernel(tc, x_words, x_scales, w1, w2, pe, offs, ou
             nc.vector.tensor_copy(grouped[z, 0][:].rearrange("p t m j -> p m t j"), src[:, :, 0:2, :])
             nc.scalar.copy(grouped[z, 1][:].rearrange("p t m j -> p m t j"), src[:, :, 2:4, :])
             if z == 0:
-                load_pe(1)
                 load_pe(2)
                 load_pe(3)
         w1_mx = {}
@@ -101,8 +101,8 @@ def tile_picked_posadd_gelu_p_kernel(tc, x_words, x_scales, w1, w2, pe, offs, ou
         w2_raw = sb.tile([P, PACK, N], F32, name="w2_raw", tag="slot_w2", align_bytes=64)
         nc.sync.dma_start(w2_raw[:], w2.rearrange("(p j) c -> p j c", j=PACK))
 
-        proj = [sb.tile([P, S], F32, name=f"proj{t}", align_bytes=64) for t in range(PACK)]
-        for t in range(PACK):
+        proj = {t: sb.tile([P, S], F32, name=f"proj{t}", align_bytes=64) for t in (0, 2, 3)}
+        for t in proj:
             nc.scalar.copy(proj[t][:], acc[t][:])
 
         chunks = [slice(a, a + w) for a, w in zip(STARTS, WIDTHS)]
@@ -112,10 +112,14 @@ def tile_picked_posadd_gelu_p_kernel(tc, x_words, x_scales, w1, w2, pe, offs, ou
         for g, span in enumerate(spans):
             width = chunks[span.stop - 1].stop - chunks[span.start].start
             early.append(sb.tile([P, 2, width], F32, name=f"early{g}", align_bytes=64))
-        for t in range(2):
-            for g, span in enumerate(spans):
-                a, b = chunks[span.start].start, chunks[span.stop - 1].stop
-                nc.vector.tensor_tensor(early[g][:, t, :], pe_table[t][:].indirect(offsets[:, a // 16 : b // 16]), proj[t][:, a:b], ADD)
+        picked_pe = sb.tile([P, S], F32, name="picked_pe", align_bytes=64)
+        for g, span in enumerate(spans):
+            a, b = chunks[span.start].start, chunks[span.stop - 1].stop
+            entries = offsets[:, a // 16 : b // 16]
+            half = slice(g * S // 2, (g + 1) * S // 2)
+            nc.vector.tensor_copy(picked_pe[:, half], pe_pair[:, T : 2 * T].indirect(offsets[:, half.start // 16 : half.stop // 16]))
+            nc.vector.tensor_tensor(early[g][:, 0, :], pe_pair[:].indirect(entries), proj[0][:, a:b], ADD)
+            nc.vector.tensor_tensor(early[g][:, 1, :], acc[1][:, a:b], picked_pe[:, a:b], ADD)
         for g, span in enumerate(spans):
             a = chunks[span.start].start
             for c in span:
@@ -123,19 +127,13 @@ def tile_picked_posadd_gelu_p_kernel(tc, x_words, x_scales, w1, w2, pe, offs, ou
                 nc.scalar.activation(hidden[c][:, :, 0:2], part.rearrange("p t n -> p n t"), GELU)
 
         late_spans = (range(0, 1), range(1, 2), range(2, 3), range(3, 5))
-        late = []
-        for g, span in enumerate(late_spans):
-            width = chunks[span.stop - 1].stop - chunks[span.start].start
-            late.append(sb.tile([P, 2, width], F32, name=f"late{g}", align_bytes=64))
-        for t in range(2, PACK):
-            for g, span in enumerate(late_spans):
-                a, b = chunks[span.start].start, chunks[span.stop - 1].stop
-                nc.vector.tensor_tensor(late[g][:, t - 2, :], pe_table[t][:].indirect(offsets[:, a // 16 : b // 16]), proj[t][:, a:b], ADD)
-        for g, span in enumerate(late_spans):
-            a = chunks[span.start].start
-            for c in span:
-                part = late[g][:, :, chunks[c].start - a : chunks[c].stop - a]
-                nc.scalar.activation(hidden[c][:, :, 2:4], part.rearrange("p t n -> p n t"), GELU)
+        late = sb.tile([P, 2, S], F32, name="late", align_bytes=64)
+        nc.vector.tensor_tensor(late[:, 0, :], pe_table[2][:].indirect(offsets[:]), proj[2][:], ADD)
+        for span in late_spans:
+            a, b = chunks[span.start].start, chunks[span.stop - 1].stop
+            nc.vector.tensor_tensor(late[:, 1, a:b], pe_table[3][:].indirect(offsets[:, a // 16 : b // 16]), proj[3][:, a:b], ADD)
+        for c, cols in enumerate(chunks):
+            nc.scalar.activation(hidden[c][:, :, 2:4], late[:, :, cols].rearrange("p t n -> p n t"), GELU)
         w2_grouped = sb.tile([P, N, PACK], BF16, name="w2_grouped", tag="w2_grouped", align_bytes=64)
         nc.vector.tensor_copy(
             w2_grouped[:].rearrange("p (c i) j -> p c j i", i=PACK),

@@ -20,8 +20,14 @@ P = 128
 PACK = 4
 K_PASS = P * PACK
 PASSES = K // K_PASS
-WIDTHS = (64, 128, 128, 128, 64)
-STARTS = tuple(sum(WIDTHS[:c]) for c in range(len(WIDTHS)))
+ALIGN = 256
+CHUNKS = (64, 128, 128, 128, 64)
+EARLY_RUNS = (192, 320)
+LATE_RUNS = (64, 128, 128, 192)
+
+
+def cut(widths):
+    return [slice(sum(widths[:i]), sum(widths[: i + 1])) for i in range(len(widths))]
 
 
 def tile_picked_posadd_gelu_p_kernel(tc, x_words, x_scales, w1, w2, pe, offs, out):
@@ -30,61 +36,71 @@ def tile_picked_posadd_gelu_p_kernel(tc, x_words, x_scales, w1, w2, pe, offs, ou
         sb = ctx.enter_context(tc.tile_pool(name="sb", bufs=1))
         ps = ctx.enter_context(tc.psum_pool(name="ps", bufs=1))
 
-        offsets = sb.tile([P, S // 16], U16, name="offsets")
+        def tile(name, shape, dtype, buffer=None):
+            return sb.tile(shape, dtype, name=name, tag=buffer or name, align_bytes=ALIGN)
 
-        scale_table = sb.tile([P, T], U8, name="scale_table", tag="slot1", align_bytes=64)
+        offsets = tile("offsets", [P, S // 16], U16)
+
+        def entries(run):
+            return offsets[:, run.start // 16 : run.stop // 16]
+
+        scale_table = tile("scale_table", [P, T], U8, "first_plane")
         nc.scalar.dma_start(scale_table[64:96, :].bitcast(I32), x_scales.rearrange("z b c -> b z c").bitcast(I32))
         nc.vector.memset(scale_table[0:64, :].bitcast(I32), 0)
         nc.vector.memset(scale_table[96:P, :].bitcast(I32), 0)
 
-        w1_raw = [sb.tile([P, PACK, H], F32, name=f"w1_raw{z}", tag=("slot2", "slot_w2")[z], align_bytes=64) for z in range(PASSES)]
-        word_table = [sb.tile([P, T], U16, name=f"word_table{z}", tag=("slot0", "words1")[z], align_bytes=64) for z in range(PASSES)]
+        word_table = [tile(f"word_table{z}", [P, T], U16, ("second_plane", "words1")[z]) for z in range(PASSES)]
+        w1_raw = [tile(f"w1_raw{z}", [P, PACK, H], F32, ("fourth_plane", "w2_raw")[z]) for z in range(PASSES)]
         nc.sync.dma_start(word_table[0][:].bitcast(I32), x_words[0].bitcast(I32))
         nc.sync.dma_start(offsets[:], offs)
-        nc.sync.dma_start(w1_raw[0][:], w1[0:K_PASS, :].rearrange("(p j) c -> p j c", j=PACK))
-        nc.sync.dma_start(w1_raw[1][:], w1[K_PASS:K, :].rearrange("(p j) c -> p j c", j=PACK))
+        for z in range(PASSES):
+            nc.sync.dma_start(w1_raw[z][:], w1[z * K_PASS : (z + 1) * K_PASS, :].rearrange("(p j) c -> p j c", j=PACK))
         nc.sync.dma_start(word_table[1][:].bitcast(I32), x_words[1].bitcast(I32))
 
-        picked_scales = sb.tile([P, S], U8, name="picked_scales", tag="slot3", align_bytes=64)
-        x_scale = sb.tile([P, PASSES * S], U8, name="x_scale", align_bytes=64)
+        picked_scales = tile("picked_scales", [P, S], U8)
+        x_scale = tile("x_scale", [P, PASSES * S], U8)
         nc.vector.memset(x_scale[:].bitcast(I32), 0)
         nc.vector.tensor_copy(picked_scales[:], scale_table[:].indirect(offsets[:]))
         for q in range(4):
-            nc.scalar.dma_start(x_scale[32 * q : 32 * q + 4, :].bitcast(I32), picked_scales[64 + 8 * q : 64 + 8 * q + 8, :].bitcast(I32))
-        x_code = [sb.tile([P, S], U16, name=f"x_code{z}", align_bytes=64) for z in range(PASSES)]
-        nc.vector.tensor_copy(x_code[0][:], word_table[0][:].indirect(offsets[:]))
+            nc.sync.dma_start(x_scale[32 * q : 32 * q + 4, :].bitcast(I32), picked_scales[64 + 8 * q : 64 + 8 * q + 8, :].bitcast(I32))
+
         pe_rows = pe.rearrange("(p t) c -> t p c", t=PACK)
         pe_table = {}
 
-        def load_pe(t):
-            pe_table[t] = sb.tile([P, T], F32, name=f"pe_table{t}", tag=f"slot{t}", align_bytes=64)
+        def load_plane(t, buffer):
+            pe_table[t] = tile(f"pe_table{t}", [P, T], F32, buffer)
             nc.sync.dma_start(pe_table[t][:], pe_rows[t])
 
-        pe_pair = sb.tile([P, 2 * T], F32, name="pe_pair", tag="slot0", align_bytes=64)
-        nc.sync.dma_start(pe_pair[:], pe.rearrange("(p t) c -> p (t c)", t=PACK)[:, 0 : 2 * T])
-        warm = sb.tile([P, 1], F32, name="warm", align_bytes=64)
+        load_plane(0, "first_plane")
+        x_code = [tile(f"x_code{z}", [P, S], U16) for z in range(PASSES)]
+        nc.vector.tensor_copy(x_code[0][:], word_table[0][:].indirect(offsets[:]))
+        load_plane(1, "second_plane")
+
+        warm = tile("warm", [P, 1], F32)
         nc.scalar.activation(warm[:], w1_raw[0][:, 0, 0:1], GELU)
-        acc = [ps.tile([P, S], F32, name=f"acc{t}", tag=f"bank{t}") for t in range(PACK)]
+
         grouped = {}
         for z in range(PASSES):
-            src = w1_raw[z][:].rearrange("p j (m t) -> p m t j", t=PACK)
+            columns = w1_raw[z][:].rearrange("p j (m t) -> p m t j", t=PACK)
             for u in range(2):
-                grouped[z, u] = sb.tile([P, 2, P, PACK], BF16, name=f"w1_grouped{z}{u}", align_bytes=64)
-            nc.vector.tensor_copy(grouped[z, 0][:].rearrange("p t m j -> p m t j"), src[:, :, 0:2, :])
-            nc.scalar.copy(grouped[z, 1][:].rearrange("p t m j -> p m t j"), src[:, :, 2:4, :])
-            if z == 0:
-                load_pe(2)
-                load_pe(3)
+                grouped[z, u] = tile(f"w1_grouped{z}{u}", [P, 2, P, PACK], BF16, "third_plane" if (z, u) == (0, 0) else None)
+            nc.vector.tensor_copy(grouped[z, 0][:].rearrange("p t m j -> p m t j"), columns[:, :, 0:2, :])
+            nc.scalar.copy(grouped[z, 1][:].rearrange("p t m j -> p m t j"), columns[:, :, 2:4, :])
         w1_mx = {}
         for u in range(2):
             for z in range(PASSES):
-                tag = "words1" if (z, u) == (0, 1) else f"w1_codes{z}{u}"
-                codes = sb.tile([P, 2 * P], U32, name=f"w1_codes{z}{u}", tag=tag, align_bytes=64)
-                scales = sb.tile([P, 2 * P], U8, name=f"w1_scales{z}{u}", align_bytes=64)
+                codes = tile(f"w1_codes{z}{u}", [P, 2 * P], U32, "words1" if (z, u) == (0, 1) else None)
+                scales = tile(f"w1_scales{z}{u}", [P, 2 * P], U8)
                 nc.vector.quantize_mx(codes[:].bitcast(FP8X4), scales[:], grouped[z, u][:].rearrange("p t m j -> p (t m j)"))
                 w1_mx[z, u] = (codes, scales)
             if u == 0:
                 nc.vector.tensor_copy(x_code[1][:], word_table[1][:].indirect(offsets[:]))
+        load_plane(2, "third_plane")
+        load_plane(3, "fourth_plane")
+        w2_raw = tile("w2_raw", [P, PACK, N], F32)
+        nc.sync.dma_start(w2_raw[:], w2.rearrange("(p j) c -> p j c", j=PACK))
+
+        acc = [ps.tile([P, S], F32, name=f"acc{t}", tag=f"bank{t}") for t in range(PACK)]
         for t in range(PACK):
             for z in range(PASSES):
                 codes, scales = w1_mx[z, t // 2]
@@ -98,51 +114,37 @@ def tile_picked_posadd_gelu_p_kernel(tc, x_words, x_scales, w1, w2, pe, offs, ou
                     start=(z == 0),
                     stop=(z == PASSES - 1),
                 )
-        w2_raw = sb.tile([P, PACK, N], F32, name="w2_raw", tag="slot_w2", align_bytes=64)
-        nc.sync.dma_start(w2_raw[:], w2.rearrange("(p j) c -> p j c", j=PACK))
-
-        proj = {t: sb.tile([P, S], F32, name=f"proj{t}", align_bytes=64) for t in (0, 2, 3)}
-        for t in proj:
+        proj = [tile(f"proj{t}", [P, S], F32) for t in range(PACK)]
+        for t in range(PACK):
             nc.scalar.copy(proj[t][:], acc[t][:])
 
-        chunks = [slice(a, a + w) for a, w in zip(STARTS, WIDTHS)]
-        hidden = [sb.tile([P, w, PACK], BF16, name=f"hidden{c}", align_bytes=64) for c, w in enumerate(WIDTHS)]
-        spans = (range(0, 2), range(2, len(WIDTHS)))
-        early = []
-        for g, span in enumerate(spans):
-            width = chunks[span.stop - 1].stop - chunks[span.start].start
-            early.append(sb.tile([P, 2, width], F32, name=f"early{g}", align_bytes=64))
-        picked_pe = sb.tile([P, S], F32, name="picked_pe", align_bytes=64)
-        for g, span in enumerate(spans):
-            a, b = chunks[span.start].start, chunks[span.stop - 1].stop
-            entries = offsets[:, a // 16 : b // 16]
-            half = slice(g * S // 2, (g + 1) * S // 2)
-            nc.vector.tensor_copy(picked_pe[:, half], pe_pair[:, T : 2 * T].indirect(offsets[:, half.start // 16 : half.stop // 16]))
-            nc.vector.tensor_tensor(early[g][:, 0, :], pe_pair[:].indirect(entries), proj[0][:, a:b], ADD)
-            nc.vector.tensor_tensor(early[g][:, 1, :], acc[1][:, a:b], picked_pe[:, a:b], ADD)
-        for g, span in enumerate(spans):
-            a = chunks[span.start].start
-            for c in span:
-                part = early[g][:, :, chunks[c].start - a : chunks[c].stop - a]
-                nc.scalar.activation(hidden[c][:, :, 0:2], part.rearrange("p t n -> p n t"), GELU)
+        chunks = cut(CHUNKS)
+        hidden = [tile(f"hidden{c}", [P, w, PACK], BF16) for c, w in enumerate(CHUNKS)]
 
-        late_spans = (range(0, 1), range(1, 2), range(2, 3), range(3, 5))
-        late = sb.tile([P, 2, S], F32, name="late", align_bytes=64)
-        nc.vector.tensor_tensor(late[:, 0, :], pe_table[2][:].indirect(offsets[:]), proj[2][:], ADD)
-        for span in late_spans:
-            a, b = chunks[span.start].start, chunks[span.stop - 1].stop
-            nc.vector.tensor_tensor(late[:, 1, a:b], pe_table[3][:].indirect(offsets[:, a // 16 : b // 16]), proj[3][:, a:b], ADD)
-        for c, cols in enumerate(chunks):
-            nc.scalar.activation(hidden[c][:, :, 2:4], late[:, :, cols].rearrange("p t n -> p n t"), GELU)
-        w2_grouped = sb.tile([P, N, PACK], BF16, name="w2_grouped", tag="w2_grouped", align_bytes=64)
+        def add_planes(name, first, widths):
+            runs = cut(widths)
+            sums = [tile(f"{name}{r}", [P, 2, w], F32) for r, w in enumerate(widths)]
+            for t in range(2):
+                for run, total in zip(runs, sums):
+                    nc.vector.tensor_tensor(total[:, t, :], pe_table[first + t][:].indirect(entries(run)), proj[first + t][:, run], ADD)
+            for run, total in zip(runs, sums):
+                for c, cols in enumerate(chunks):
+                    if run.start <= cols.start < run.stop:
+                        part = total[:, :, cols.start - run.start : cols.stop - run.start]
+                        nc.scalar.activation(hidden[c][:, :, first : first + 2], part.rearrange("p t n -> p n t"), GELU)
+
+        add_planes("early", 0, EARLY_RUNS)
+        add_planes("late", 2, LATE_RUNS)
+
+        w2_grouped = tile("w2_grouped", [P, N, PACK], BF16)
         nc.vector.tensor_copy(
             w2_grouped[:].rearrange("p (c i) j -> p c j i", i=PACK),
             w2_raw[:].rearrange("p j (c i) -> p c j i", i=PACK),
         )
-        w2_codes = sb.tile([P, N], U32, name="w2_codes", align_bytes=64)
-        w2_scales = sb.tile([P, N], U8, name="w2_scales", align_bytes=64)
-        h_codes = [sb.tile([P, w], U32, name=f"h_codes{c}", align_bytes=64) for c, w in enumerate(WIDTHS)]
-        h_scales = [sb.tile([P, w], U8, name=f"h_scales{c}", align_bytes=64) for c, w in enumerate(WIDTHS)]
+        w2_codes = tile("w2_codes", [P, N], U32)
+        w2_scales = tile("w2_scales", [P, N], U8)
+        h_codes = [tile(f"h_codes{c}", [P, w], U32) for c, w in enumerate(CHUNKS)]
+        h_scales = [tile(f"h_scales{c}", [P, w], U8) for c, w in enumerate(CHUNKS)]
 
         def quantise_h(c):
             nc.vector.quantize_mx(h_codes[c][:].bitcast(FP8X4), h_scales[c][:], hidden[c][:].rearrange("p n t -> p (n t)"))
@@ -150,11 +152,11 @@ def tile_picked_posadd_gelu_p_kernel(tc, x_words, x_scales, w1, w2, pe, offs, ou
         quantise_h(0)
         quantise_h(1)
         nc.vector.quantize_mx(w2_codes[:].bitcast(FP8X4), w2_scales[:], w2_grouped[:].rearrange("p c j -> p (c j)"))
-        for c in range(2, len(WIDTHS)):
+        for c in range(2, len(CHUNKS)):
             quantise_h(c)
 
         result = []
-        for c, w in enumerate(WIDTHS):
+        for c, w in enumerate(CHUNKS):
             res = ps.tile([P, w], F32, name=f"res{c}", tag=f"bank{(PACK + c) % 8}")
             nc.tensor.matmul_mx(
                 res[:],
@@ -167,7 +169,7 @@ def tile_picked_posadd_gelu_p_kernel(tc, x_words, x_scales, w1, w2, pe, offs, ou
             )
             result.append(res)
         for c, cols in enumerate(chunks):
-            staged = sb.tile([P, WIDTHS[c]], F32, name=f"staged{c}", align_bytes=64)
+            staged = tile(f"staged{c}", [P, CHUNKS[c]], F32)
             if c == len(chunks) - 1:
                 nc.vector.tensor_copy(staged[:], result[c][:])
             else:

@@ -22,40 +22,39 @@ K_PASS = P * PACK
 PASSES = K // K_PASS
 ALIGN = 256
 CHUNKS = (64, 128, 128, 128, 64)
-EARLY_RUNS = (192, 320)
-LATE_RUNS = (64, 128, 128, 192)
-
-
-def cut(widths):
-    return [slice(sum(widths[:i]), sum(widths[: i + 1])) for i in range(len(widths))]
+STARTS = (448, 0, 128, 256, 384)
+EARLY_RUNS = (slice(0, 256), slice(256, 512))
+LATE_RUNS = (slice(448, 512), slice(0, 128), slice(128, 256), slice(256, 448))
 
 
 def tile_picked_posadd_gelu_p_kernel(tc, x_words, x_scales, w1, w2, pe, offs, out):
     nc = tc.nc
     with ExitStack() as ctx:
         sb = ctx.enter_context(tc.tile_pool(name="sb", bufs=1))
+        shared = ctx.enter_context(tc.tile_pool(name="shared", bufs=1))
         ps = ctx.enter_context(tc.psum_pool(name="ps", bufs=1))
 
         def tile(name, shape, dtype, buffer=None):
             return sb.tile(shape, dtype, name=name, tag=buffer or name, align_bytes=ALIGN)
+
+        def placed(name, shape, dtype, offset):
+            return shared.tile(shape, dtype, name=name, offset=offset, align_bytes=ALIGN)
 
         offsets = tile("offsets", [P, S // 16], U16)
 
         def entries(run):
             return offsets[:, run.start // 16 : run.stop // 16]
 
-        scale_table = tile("scale_table", [P, T], U8, "first_plane")
+        scale_table = placed("scale_table", [P, T], U8, 8192)
         nc.scalar.dma_start(scale_table[64:96, :].bitcast(I32), x_scales.rearrange("z b c -> b z c").bitcast(I32))
         nc.vector.memset(scale_table[0:64, :].bitcast(I32), 0)
         nc.vector.memset(scale_table[96:P, :].bitcast(I32), 0)
 
-        word_table = [tile(f"word_table{z}", [P, T], U16, ("second_plane", "words1")[z]) for z in range(PASSES)]
-        w1_raw = [tile(f"w1_raw{z}", [P, PACK, H], F32, ("fourth_plane", "w2_raw")[z]) for z in range(PASSES)]
-        nc.sync.dma_start(word_table[0][:].bitcast(I32), x_words[0].bitcast(I32))
+        both_words = tile("both_words", [P, PASSES * T], U16, "third_plane")
+        w1_raw = tile("w1_raw", [P, PASSES, PACK, H], F32, "w2_raw")
+        nc.sync.dma_start(both_words[:].bitcast(I32).rearrange("p (z c) -> p z c", z=PASSES), x_words.rearrange("z p c -> p z c").bitcast(I32))
         nc.sync.dma_start(offsets[:], offs)
-        for z in range(PASSES):
-            nc.sync.dma_start(w1_raw[z][:], w1[z * K_PASS : (z + 1) * K_PASS, :].rearrange("(p j) c -> p j c", j=PACK))
-        nc.sync.dma_start(word_table[1][:].bitcast(I32), x_words[1].bitcast(I32))
+        nc.sync.dma_start(w1_raw[:].rearrange("p z j c -> p z (j c)"), w1.rearrange("(z p j) c -> p z (j c)", z=PASSES, j=PACK))
 
         picked_scales = tile("picked_scales", [P, S], U8)
         x_scale = tile("x_scale", [P, PASSES * S], U8)
@@ -65,38 +64,34 @@ def tile_picked_posadd_gelu_p_kernel(tc, x_words, x_scales, w1, w2, pe, offs, ou
             nc.sync.dma_start(x_scale[32 * q : 32 * q + 4, :].bitcast(I32), picked_scales[64 + 8 * q : 64 + 8 * q + 8, :].bitcast(I32))
 
         pe_rows = pe.rearrange("(p t) c -> t p c", t=PACK)
-        pe_table = {}
-
-        def load_plane(t, buffer):
-            pe_table[t] = tile(f"pe_table{t}", [P, T], F32, buffer)
+        pe_pair = placed("pe_pair", [P, 2 * T], F32, 9216)
+        nc.sync.dma_start(pe_pair[:], pe.rearrange("(p t) c -> p (t c)", t=PACK)[:, 0 : 2 * T])
+        x_code = [tile(f"x_code{z}", [P, S], U16) for z in range(PASSES)]
+        nc.vector.tensor_copy(x_code[0][:], both_words[:].indirect(offsets[:]))
+        second_words = placed("second_words", [P, T], U16, 5120)
+        nc.vector.tensor_copy(second_words[:].bitcast(I32), both_words[:, T : 2 * T].bitcast(I32))
+        nc.vector.tensor_copy(x_code[1][:], second_words[:].indirect(offsets[:]))
+        pe_table = {2: tile("pe_table2", [P, T], F32, "third_plane"), 3: placed("pe_table3", [P, T], F32, 1024)}
+        for t in pe_table:
             nc.sync.dma_start(pe_table[t][:], pe_rows[t])
 
-        load_plane(0, "first_plane")
-        x_code = [tile(f"x_code{z}", [P, S], U16) for z in range(PASSES)]
-        nc.vector.tensor_copy(x_code[0][:], word_table[0][:].indirect(offsets[:]))
-        load_plane(1, "second_plane")
-
         warm = tile("warm", [P, 1], F32)
-        nc.scalar.activation(warm[:], w1_raw[0][:, 0, 0:1], GELU)
+        nc.scalar.activation(warm[:], w1_raw[:, 0, 0, 0:1], GELU)
 
         grouped = {}
         for z in range(PASSES):
-            columns = w1_raw[z][:].rearrange("p j (m t) -> p m t j", t=PACK)
+            columns = w1_raw[:, z].rearrange("p j (m t) -> p m t j", t=PACK)
             for u in range(2):
-                grouped[z, u] = tile(f"w1_grouped{z}{u}", [P, 2, P, PACK], BF16, "third_plane" if (z, u) == (0, 0) else None)
+                grouped[z, u] = tile(f"w1_grouped{z}{u}", [P, 2, P, PACK], BF16)
             nc.vector.tensor_copy(grouped[z, 0][:].rearrange("p t m j -> p m t j"), columns[:, :, 0:2, :])
             nc.scalar.copy(grouped[z, 1][:].rearrange("p t m j -> p m t j"), columns[:, :, 2:4, :])
         w1_mx = {}
         for u in range(2):
             for z in range(PASSES):
-                codes = tile(f"w1_codes{z}{u}", [P, 2 * P], U32, "words1" if (z, u) == (0, 1) else None)
+                codes = tile(f"w1_codes{z}{u}", [P, 2 * P], U32)
                 scales = tile(f"w1_scales{z}{u}", [P, 2 * P], U8)
                 nc.vector.quantize_mx(codes[:].bitcast(FP8X4), scales[:], grouped[z, u][:].rearrange("p t m j -> p (t m j)"))
                 w1_mx[z, u] = (codes, scales)
-            if u == 0:
-                nc.vector.tensor_copy(x_code[1][:], word_table[1][:].indirect(offsets[:]))
-        load_plane(2, "third_plane")
-        load_plane(3, "fourth_plane")
         w2_raw = tile("w2_raw", [P, PACK, N], F32)
         nc.sync.dma_start(w2_raw[:], w2.rearrange("(p j) c -> p j c", j=PACK))
 
@@ -114,27 +109,31 @@ def tile_picked_posadd_gelu_p_kernel(tc, x_words, x_scales, w1, w2, pe, offs, ou
                     start=(z == 0),
                     stop=(z == PASSES - 1),
                 )
-        proj = [tile(f"proj{t}", [P, S], F32) for t in range(PACK)]
-        for t in range(PACK):
+        proj = {t: tile(f"proj{t}", [P, S], F32) for t in (0, 2, 3)}
+        for t in proj:
             nc.scalar.copy(proj[t][:], acc[t][:])
 
-        chunks = cut(CHUNKS)
+        chunks = [slice(a, a + w) for a, w in zip(STARTS, CHUNKS)]
         hidden = [tile(f"hidden{c}", [P, w, PACK], BF16) for c, w in enumerate(CHUNKS)]
 
-        def add_planes(name, first, widths):
-            runs = cut(widths)
-            sums = [tile(f"{name}{r}", [P, 2, w], F32) for r, w in enumerate(widths)]
-            for t in range(2):
-                for run, total in zip(runs, sums):
-                    nc.vector.tensor_tensor(total[:, t, :], pe_table[first + t][:].indirect(entries(run)), proj[first + t][:, run], ADD)
-            for run, total in zip(runs, sums):
-                for c, cols in enumerate(chunks):
-                    if run.start <= cols.start < run.stop:
-                        part = total[:, :, cols.start - run.start : cols.stop - run.start]
-                        nc.scalar.activation(hidden[c][:, :, first : first + 2], part.rearrange("p t n -> p n t"), GELU)
+        def gelu_pair(c, first, sums):
+            nc.scalar.activation(hidden[c][:, :, first : first + 2], sums[:, :, chunks[c]].rearrange("p t n -> p n t"), GELU)
 
-        add_planes("early", 0, EARLY_RUNS)
-        add_planes("late", 2, LATE_RUNS)
+        picked_pe = tile("picked_pe", [P, S], F32)
+        early = tile("early", [P, 2, S], F32)
+        nc.vector.tensor_copy(picked_pe[:], pe_pair[:, T : 2 * T].indirect(offsets[:]))
+        for run in EARLY_RUNS:
+            nc.vector.tensor_tensor(early[:, 0, run], pe_pair[:].indirect(entries(run)), proj[0][:, run], ADD)
+            nc.vector.tensor_tensor(early[:, 1, run], acc[1][:, run], picked_pe[:, run], ADD)
+        for c in (1, 2, 3, 0, 4):
+            gelu_pair(c, 0, early)
+
+        late = tile("late", [P, 2, S], F32)
+        nc.vector.tensor_tensor(late[:, 0, :], pe_table[2][:].indirect(offsets[:]), proj[2][:], ADD)
+        for run in LATE_RUNS:
+            nc.vector.tensor_tensor(late[:, 1, run], pe_table[3][:].indirect(entries(run)), proj[3][:, run], ADD)
+        for c in range(len(CHUNKS)):
+            gelu_pair(c, 2, late)
 
         w2_grouped = tile("w2_grouped", [P, N, PACK], BF16)
         nc.vector.tensor_copy(
@@ -168,11 +167,12 @@ def tile_picked_posadd_gelu_p_kernel(tc, x_words, x_scales, w1, w2, pe, offs, ou
                 stop=True,
             )
             result.append(res)
-        for c, cols in enumerate(chunks):
+        ends = tile("staged_ends", [P, 2, CHUNKS[0]], F32)
+        nc.scalar.copy(ends[:, 1, :], result[0][:])
+        for c in (1, 2, 3):
             staged = tile(f"staged{c}", [P, CHUNKS[c]], F32)
-            if c == len(chunks) - 1:
-                nc.vector.tensor_copy(staged[:], result[c][:])
-            else:
-                nc.scalar.copy(staged[:], result[c][:])
-            queue = nc.scalar if c == len(chunks) - 2 else nc.sync
-            queue.dma_start(out[:, cols], staged[:])
+            nc.scalar.copy(staged[:], result[c][:])
+            queue = nc.scalar if c == 3 else nc.sync
+            queue.dma_start(out[:, chunks[c]], staged[:])
+        nc.vector.tensor_copy(ends[:, 0, :], result[4][:])
+        nc.sync.dma_start(out[:, STARTS[4] : S], ends[:].rearrange("p c n -> p (c n)"))

@@ -60,7 +60,7 @@ def tile_picked_posadd_gelu_p_kernel(tc, x_words, x_scales, w1, w2, pe, offs, ou
         x_scale = tile("x_scale", [P, PASSES * S], U8)
         nc.vector.memset(x_scale[:].bitcast(I32), 0)
         nc.vector.tensor_copy(picked_scales[:], scale_table[:].indirect(offsets[:]))
-        for q in range(4):
+        for q in (0, 2, 1, 3):
             nc.sync.dma_start(x_scale[32 * q : 32 * q + 4, :].bitcast(I32), picked_scales[64 + 8 * q : 64 + 8 * q + 8, :].bitcast(I32))
 
         pe_rows = pe.rearrange("(p t) c -> t p c", t=PACK)

@@ -154,8 +154,9 @@ def tile_picked_posadd_gelu_p_kernel(tc, x_words, x_scales, w1, w2, pe, offs, ou
         for c in range(2, len(CHUNKS)):
             quantise_h(c)
 
-        result = []
-        for c, w in enumerate(CHUNKS):
+        result = {}
+        for c in (1, 2, 0, 3, 4):
+            w = CHUNKS[c]
             res = ps.tile([P, w], F32, name=f"res{c}", tag=f"bank{(PACK + c) % 8}")
             nc.tensor.matmul_mx(
                 res[:],
@@ -166,13 +167,15 @@ def tile_picked_posadd_gelu_p_kernel(tc, x_words, x_scales, w1, w2, pe, offs, ou
                 start=True,
                 stop=True,
             )
-            result.append(res)
+            result[c] = res
         ends = tile("staged_ends", [P, 2, CHUNKS[0]], F32)
+        staged = {c: tile(f"staged{c}", [P, CHUNKS[c]], F32) for c in (1, 2, 3)}
+        nc.scalar.copy(staged[1][:], result[1][:])
+        nc.sync.dma_start(out[:, chunks[1]], staged[1][:])
+        nc.vector.tensor_copy(staged[2][:], result[2][:])
+        nc.sync.dma_start(out[:, chunks[2]], staged[2][:])
         nc.scalar.copy(ends[:, 1, :], result[0][:])
-        for c in (1, 2, 3):
-            staged = tile(f"staged{c}", [P, CHUNKS[c]], F32)
-            nc.scalar.copy(staged[:], result[c][:])
-            queue = nc.scalar if c == 3 else nc.sync
-            queue.dma_start(out[:, chunks[c]], staged[:])
+        nc.scalar.copy(staged[3][:], result[3][:])
+        nc.scalar.dma_start(out[:, chunks[3]], staged[3][:])
         nc.vector.tensor_copy(ends[:, 0, :], result[4][:])
         nc.sync.dma_start(out[:, STARTS[4] : S], ends[:].rearrange("p c n -> p (c n)"))

@@ -23,6 +23,7 @@ PASSES = K // K_PASS
 ALIGN = 256
 CHUNKS = (64, 128, 128, 128, 64)
 STARTS = (448, 0, 128, 256, 384)
+WOVEN = 1
 EARLY_RUNS = (slice(0, 256), slice(256, 512))
 LATE_RUNS = (slice(448, 512), slice(0, 128), slice(128, 256), slice(256, 448))
 
@@ -116,6 +117,8 @@ def tile_picked_posadd_gelu_p_kernel(tc, x_words, x_scales, w1, w2, pe, offs, ou
         chunks = [slice(a, a + w) for a, w in zip(STARTS, CHUNKS)]
         hidden = [tile(f"hidden{c}", [P, w, PACK], BF16) for c, w in enumerate(CHUNKS)]
 
+        pairs = tile("pairs", [P, 2, CHUNKS[WOVEN], 2], BF16)
+
         def gelu_pair(c, first, sums):
             nc.scalar.activation(hidden[c][:, :, first : first + 2], sums[:, :, chunks[c]].rearrange("p t n -> p n t"), GELU)
 
@@ -126,19 +129,30 @@ def tile_picked_posadd_gelu_p_kernel(tc, x_words, x_scales, w1, w2, pe, offs, ou
             nc.vector.tensor_tensor(early[:, 0, run], pe_pair[:].indirect(entries(run)), proj[0][:, run], ADD)
             nc.vector.tensor_tensor(early[:, 1, run], acc[1][:, run], picked_pe[:, run], ADD)
         for c in (1, 2, 3, 0, 4):
-            gelu_pair(c, 0, early)
+            if c == WOVEN:
+                nc.scalar.activation(pairs[:, 0], early[:, :, chunks[c]].rearrange("p t n -> p n t"), GELU)
+            else:
+                gelu_pair(c, 0, early)
 
         late = tile("late", [P, 2, S], F32)
         nc.vector.tensor_tensor(late[:, 0, :], pe_table[2][:].indirect(offsets[:]), proj[2][:], ADD)
+        nc.scalar.activation(pairs[:, 1, :, 0], late[:, 0, chunks[WOVEN]], GELU)
         for run in LATE_RUNS:
             nc.vector.tensor_tensor(late[:, 1, run], pe_table[3][:].indirect(entries(run)), proj[3][:, run], ADD)
         for c in range(len(CHUNKS)):
-            gelu_pair(c, 2, late)
+            if c == WOVEN:
+                nc.scalar.activation(pairs[:, 1, :, 1], late[:, 1, chunks[c]], GELU)
+            else:
+                gelu_pair(c, 2, late)
 
         w2_grouped = tile("w2_grouped", [P, N, PACK], BF16)
         nc.vector.tensor_copy(
             w2_grouped[:].rearrange("p (c i) j -> p c j i", i=PACK),
             w2_raw[:].rearrange("p j (c i) -> p c j i", i=PACK),
+        )
+        nc.vector.tensor_copy(
+            hidden[WOVEN][:].rearrange("p n t -> p (n t)").bitcast(F32).rearrange("p (n u) -> p n u", u=2),
+            pairs[:].rearrange("p u n t -> p (u n t)").bitcast(F32).rearrange("p (u n) -> p n u", u=2),
         )
         w2_codes = tile("w2_codes", [P, N], U32)
         w2_scales = tile("w2_scales", [P, N], U8)
@@ -148,9 +162,9 @@ def tile_picked_posadd_gelu_p_kernel(tc, x_words, x_scales, w1, w2, pe, offs, ou
         def quantise_h(c):
             nc.vector.quantize_mx(h_codes[c][:].bitcast(FP8X4), h_scales[c][:], hidden[c][:].rearrange("p n t -> p (n t)"))
 
+        nc.vector.quantize_mx(w2_codes[:].bitcast(FP8X4), w2_scales[:], w2_grouped[:].rearrange("p c j -> p (c j)"))
         quantise_h(0)
         quantise_h(1)
-        nc.vector.quantize_mx(w2_codes[:].bitcast(FP8X4), w2_scales[:], w2_grouped[:].rearrange("p c j -> p (c j)"))
         for c in range(2, len(CHUNKS)):
             quantise_h(c)
 

@@ -14,6 +14,7 @@ U8 = mybir.dt.uint8
 FP8X4 = mybir.dt.float8_e4m3fn_x4
 FP4X4 = mybir.dt.float4_e2m1fn_x4
 GELU = mybir.ActivationFunctionType.Gelu_apprx_tanh
+COPY = mybir.ActivationFunctionType.Copy
 ADD = mybir.AluOpType.add
 
 P = 128
@@ -25,7 +26,8 @@ CHUNKS = (64, 128, 128, 128, 64)
 STARTS = (448, 0, 128, 256, 384)
 WOVEN = 1
 EARLY_RUNS = (slice(0, 256), slice(256, 512))
-LATE_RUNS = (slice(448, 512), slice(0, 128), slice(128, 256), slice(256, 448))
+LATE_RUNS = (slice(448, 512), slice(0, 128), slice(128, 256), slice(256, 320))
+SCALAR_RUN = slice(320, 448)
 
 
 def tile_picked_posadd_gelu_p_kernel(tc, x_words, x_scales, w1, w2, pe, offs, out):
@@ -111,8 +113,10 @@ def tile_picked_posadd_gelu_p_kernel(tc, x_words, x_scales, w1, w2, pe, offs, ou
                     stop=(z == PASSES - 1),
                 )
         proj = {t: tile(f"proj{t}", [P, S], F32) for t in (0, 2, 3)}
-        for t in proj:
+        for t in (0, 2):
             nc.scalar.copy(proj[t][:], acc[t][:])
+        for run in (slice(0, SCALAR_RUN.start), slice(SCALAR_RUN.stop, S)):
+            nc.scalar.copy(proj[3][:, run], acc[3][:, run])
 
         chunks = [slice(a, a + w) for a, w in zip(STARTS, CHUNKS)]
         hidden = [tile(f"hidden{c}", [P, w, PACK], BF16) for c, w in enumerate(CHUNKS)]
@@ -136,12 +140,14 @@ def tile_picked_posadd_gelu_p_kernel(tc, x_words, x_scales, w1, w2, pe, offs, ou
 
         late = tile("late", [P, 2, S], F32)
         nc.vector.tensor_tensor(late[:, 0, :], pe_table[2][:].indirect(offsets[:]), proj[2][:], ADD)
-        nc.scalar.activation(pairs[:, 1, :, 0], late[:, 0, chunks[WOVEN]], GELU)
+        picked_late = tile("picked_late", [P, SCALAR_RUN.stop - SCALAR_RUN.start], F32)
+        nc.scalar.activation(picked_late[:], pe_table[3][:].indirect(entries(SCALAR_RUN)), COPY)
         for run in LATE_RUNS:
             nc.vector.tensor_tensor(late[:, 1, run], pe_table[3][:].indirect(entries(run)), proj[3][:, run], ADD)
+        nc.vector.tensor_tensor(late[:, 1, SCALAR_RUN], acc[3][:, SCALAR_RUN], picked_late[:], ADD)
         for c in range(len(CHUNKS)):
             if c == WOVEN:
-                nc.scalar.activation(pairs[:, 1, :, 1], late[:, 1, chunks[c]], GELU)
+                nc.scalar.activation(pairs[:, 1], late[:, :, chunks[c]].rearrange("p t n -> p n t"), GELU)
             else:
                 gelu_pair(c, 2, late)
 

@@ -26,8 +26,8 @@ CHUNKS = (64, 128, 128, 128, 64)
 STARTS = (448, 0, 128, 256, 384)
 WOVEN = 1
 EARLY_RUNS = (slice(0, 256), slice(256, 512))
-LATE_RUNS = (slice(448, 512), slice(0, 128), slice(128, 256), slice(256, 320))
-SCALAR_RUN = slice(320, 448)
+LATE_RUNS = (slice(448, 512), slice(0, 128), slice(128, 256))
+SCALAR_RUN = slice(256, 448)
 
 
 def tile_picked_posadd_gelu_p_kernel(tc, x_words, x_scales, w1, w2, pe, offs, out):
@@ -168,8 +168,8 @@ def tile_picked_posadd_gelu_p_kernel(tc, x_words, x_scales, w1, w2, pe, offs, ou
         def quantise_h(c):
             nc.vector.quantize_mx(h_codes[c][:].bitcast(FP8X4), h_scales[c][:], hidden[c][:].rearrange("p n t -> p (n t)"))
 
-        nc.vector.quantize_mx(w2_codes[:].bitcast(FP8X4), w2_scales[:], w2_grouped[:].rearrange("p c j -> p (c j)"))
         quantise_h(0)
+        nc.vector.quantize_mx(w2_codes[:].bitcast(FP8X4), w2_scales[:], w2_grouped[:].rearrange("p c j -> p (c j)"))
         quantise_h(1)
         for c in range(2, len(CHUNKS)):
             quantise_h(c)

@@ -78,8 +78,9 @@ def tile_picked_posadd_gelu_p_kernel(tc, x_words, x_scales, w1, w2, pe, offs, ou
         for t in pe_table:
             nc.sync.dma_start(pe_table[t][:], pe_rows[t])
 
-        warm = tile("warm", [P, 1], F32)
-        nc.scalar.activation(warm[:], w1_raw[:, 0, 0, 0:1], GELU)
+        warm = tile("warm", [P, 16], F32)
+        nc.vector.memset(warm[:, 0:8], 0.0)
+        nc.scalar.activation(warm[:, 8:9], warm[:, 0:1], GELU)
 
         grouped = {}
         for z in range(PASSES):

@@ -49,13 +49,12 @@ def tile_picked_posadd_gelu_p_kernel(tc, x_words, x_scales, w1, w2, pe, offs, ou
             return offsets[:, run.start // 16 : run.stop // 16]
 
         scale_table = placed("scale_table", [P, T], U8, 8192)
-        nc.scalar.dma_start(scale_table[64:96, :].bitcast(I32), x_scales.rearrange("z b c -> b z c").bitcast(I32))
-        nc.vector.memset(scale_table[0:64, :].bitcast(I32), 0)
-        nc.vector.memset(scale_table[96:P, :].bitcast(I32), 0)
+        nc.vector.memset(scale_table[:].bitcast(I32), 0)
 
         both_words = tile("both_words", [P, PASSES * T], U16, "third_plane")
         w1_raw = tile("w1_raw", [P, PASSES, PACK, H], F32, "w2_raw")
         nc.sync.dma_start(both_words[:].bitcast(I32).rearrange("p (z c) -> p z c", z=PASSES), x_words.rearrange("z p c -> p z c").bitcast(I32))
+        nc.sync.dma_start(scale_table[0:P:4, :].bitcast(I32), x_scales.rearrange("z b c -> b z c").bitcast(I32))
         nc.sync.dma_start(offsets[:], offs)
         nc.sync.dma_start(w1_raw[:].rearrange("p z j c -> p z (j c)"), w1.rearrange("(z p j) c -> p z (j c)", z=PASSES, j=PACK))
 
@@ -64,7 +63,7 @@ def tile_picked_posadd_gelu_p_kernel(tc, x_words, x_scales, w1, w2, pe, offs, ou
         nc.vector.memset(x_scale[:].bitcast(I32), 0)
         nc.vector.tensor_copy(picked_scales[:], scale_table[:].indirect(offsets[:]))
         for q in (0, 2, 1, 3):
-            nc.sync.dma_start(x_scale[32 * q : 32 * q + 4, :].bitcast(I32), picked_scales[64 + 8 * q : 64 + 8 * q + 8, :].bitcast(I32))
+            nc.sync.dma_start(x_scale[32 * q : 32 * q + 4, :].bitcast(I32), picked_scales[32 * q : 32 * q + 32 : 4, :].bitcast(I32))
 
         pe_rows = pe.rearrange("(p t) c -> t p c", t=PACK)
         pe_pair = placed("pe_pair", [P, 2 * T], F32, 9216)
@@ -192,7 +191,7 @@ def tile_picked_posadd_gelu_p_kernel(tc, x_words, x_scales, w1, w2, pe, offs, ou
         ends = tile("staged_ends", [P, 2, CHUNKS[0]], F32)
         staged = {c: tile(f"staged{c}", [P, CHUNKS[c]], F32) for c in (1, 2, 3)}
         nc.scalar.copy(staged[1][:], result[1][:])
-        nc.sync.dma_start(out[:, chunks[1]], staged[1][:])
+        nc.scalar.dma_start(out[:, chunks[1]], staged[1][:])
         nc.vector.tensor_copy(staged[2][:], result[2][:])
         nc.sync.dma_start(out[:, chunks[2]], staged[2][:])
         nc.scalar.copy(ends[:, 1, :], result[0][:])

from contextlib import ExitStack

import concourse.mybir as mybir

K, T, S, H, N = 1024, 2048, 512, 512, 128
FLOPS = 2 * S * H * (K + N)

F32 = mybir.dt.float32
BF16 = mybir.dt.bfloat16
I32 = mybir.dt.int32
U32 = mybir.dt.uint32
U16 = mybir.dt.uint16
U8 = mybir.dt.uint8
FP8X4 = mybir.dt.float8_e4m3fn_x4
FP4X4 = mybir.dt.float4_e2m1fn_x4
GELU = mybir.ActivationFunctionType.Gelu_apprx_tanh
COPY = mybir.ActivationFunctionType.Copy
ADD = mybir.AluOpType.add

P = 128
PACK = 4
K_PASS = P * PACK
PASSES = K // K_PASS
ALIGN = 256
CHUNKS = (64, 128, 128, 128, 64)
STARTS = (448, 0, 128, 256, 384)
WOVEN = 1
EARLY_RUNS = (slice(0, 256), slice(256, 512))
LATE_RUNS = (slice(448, 512), slice(0, 128), slice(128, 256))
SCALAR_RUN = slice(256, 448)


def tile_picked_posadd_gelu_p_kernel(tc, x_words, x_scales, w1, w2, pe, offs, out):
    nc = tc.nc
    with ExitStack() as ctx:
        sb = ctx.enter_context(tc.tile_pool(name="sb", bufs=1))
        shared = ctx.enter_context(tc.tile_pool(name="shared", bufs=1))
        ps = ctx.enter_context(tc.psum_pool(name="ps", bufs=1))

        def tile(name, shape, dtype, buffer=None):
            return sb.tile(shape, dtype, name=name, tag=buffer or name, align_bytes=ALIGN)

        def placed(name, shape, dtype, offset):
            return shared.tile(shape, dtype, name=name, offset=offset, align_bytes=ALIGN)

        offsets = tile("offsets", [P, S // 16], U16)

        def entries(run):
            return offsets[:, run.start // 16 : run.stop // 16]

        scale_table = placed("scale_table", [P, T], U8, 8192)
        nc.vector.memset(scale_table[:].bitcast(I32), 0)

        both_words = tile("both_words", [P, PASSES * T], U16, "third_plane")
        w1_raw = tile("w1_raw", [P, PASSES, PACK, H], F32, "w2_raw")
        nc.sync.dma_start(both_words[:].bitcast(I32).rearrange("p (z c) -> p z c", z=PASSES), x_words.rearrange("z p c -> p z c").bitcast(I32))
        nc.sync.dma_start(scale_table[0:P:4, :].bitcast(I32), x_scales.rearrange("z b c -> b z c").bitcast(I32))
        nc.sync.dma_start(offsets[:], offs)
        nc.sync.dma_start(w1_raw[:].rearrange("p z j c -> p z (j c)"), w1.rearrange("(z p j) c -> p z (j c)", z=PASSES, j=PACK))

        picked_scales = tile("picked_scales", [P, S], U8)
        x_scale = tile("x_scale", [P, PASSES * S], U8)
        nc.vector.memset(x_scale[:].bitcast(I32), 0)
        nc.vector.tensor_copy(picked_scales[:], scale_table[:].indirect(offsets[:]))
        for q in (0, 2, 1, 3):
            nc.sync.dma_start(x_scale[32 * q : 32 * q + 4, :].bitcast(I32), picked_scales[32 * q : 32 * q + 32 : 4, :].bitcast(I32))

        pe_rows = pe.rearrange("(p t) c -> t p c", t=PACK)
        pe_pair = placed("pe_pair", [P, 2 * T], F32, 9216)
        nc.sync.dma_start(pe_pair[:], pe.rearrange("(p t) c -> p (t c)", t=PACK)[:, 0 : 2 * T])
        x_code = [tile(f"x_code{z}", [P, S], U16) for z in range(PASSES)]
        nc.vector.tensor_copy(x_code[0][:], both_words[:].indirect(offsets[:]))
        second_words = placed("second_words", [P, T], U16, 5120)
        nc.vector.tensor_copy(second_words[:].bitcast(I32), both_words[:, T : 2 * T].bitcast(I32))
        nc.vector.tensor_copy(x_code[1][:], second_words[:].indirect(offsets[:]))
        pe_table = {2: tile("pe_table2", [P, T], F32, "third_plane"), 3: placed("pe_table3", [P, T], F32, 1024)}
        for t in pe_table:
            nc.sync.dma_start(pe_table[t][:], pe_rows[t])

        warm = tile("warm", [P, 16], F32)
        nc.vector.memset(warm[:, 0:8], 0.0)
        nc.scalar.activation(warm[:, 8:9], warm[:, 0:1], GELU)

        grouped = {}
        for z in range(PASSES):
            columns = w1_raw[:, z].rearrange("p j (m t) -> p m t j", t=PACK)
            for u in range(2):
                grouped[z, u] = tile(f"w1_grouped{z}{u}", [P, 2, P, PACK], BF16)
            nc.vector.tensor_copy(grouped[z, 0][:].rearrange("p t m j -> p m t j"), columns[:, :, 0:2, :])
            nc.scalar.copy(grouped[z, 1][:].rearrange("p t m j -> p m t j"), columns[:, :, 2:4, :])
        w1_mx = {}
        for u in range(2):
            for z in range(PASSES):
                codes = tile(f"w1_codes{z}{u}", [P, 2 * P], U32)
                scales = tile(f"w1_scales{z}{u}", [P, 2 * P], U8)
                nc.vector.quantize_mx(codes[:].bitcast(FP8X4), scales[:], grouped[z, u][:].rearrange("p t m j -> p (t m j)"))
                w1_mx[z, u] = (codes, scales)
        w2_raw = tile("w2_raw", [P, PACK, N], F32)
        nc.sync.dma_start(w2_raw[:], w2.rearrange("(p j) c -> p j c", j=PACK))

        acc = [ps.tile([P, S], F32, name=f"acc{t}", tag=f"bank{t}") for t in range(PACK)]
        for t in range(PACK):
            for z in range(PASSES):
                codes, scales = w1_mx[z, t // 2]
                cols = slice(t % 2 * P, (t % 2 + 1) * P)
                nc.tensor.matmul_mx(
                    acc[t][:],
                    lhsT=codes[:, cols].bitcast(FP8X4),
                    lhsT_scale=scales[:, cols],
                    rhs=x_code[z][:].bitcast(FP4X4),
                    rhs_scale=x_scale[:, z * S : (z + 1) * S],
                    start=(z == 0),
                    stop=(z == PASSES - 1),
                )
        proj = {t: tile(f"proj{t}", [P, S], F32) for t in (0, 2, 3)}
        for t in (0, 2):
            nc.scalar.copy(proj[t][:], acc[t][:])
        for run in (slice(0, SCALAR_RUN.start), slice(SCALAR_RUN.stop, S)):
            nc.scalar.copy(proj[3][:, run], acc[3][:, run])

        chunks = [slice(a, a + w) for a, w in zip(STARTS, CHUNKS)]
        hidden = [tile(f"hidden{c}", [P, w, PACK], BF16) for c, w in enumerate(CHUNKS)]

        pairs = tile("pairs", [P, 2, CHUNKS[WOVEN], 2], BF16)

        def gelu_pair(c, first, sums):
            nc.scalar.activation(hidden[c][:, :, first : first + 2], sums[:, :, chunks[c]].rearrange("p t n -> p n t"), GELU)

        picked_pe = tile("picked_pe", [P, S], F32)
        early = tile("early", [P, 2, S], F32)
        nc.vector.tensor_copy(picked_pe[:], pe_pair[:, T : 2 * T].indirect(offsets[:]))
        for run in EARLY_RUNS:
            nc.vector.tensor_tensor(early[:, 0, run], pe_pair[:].indirect(entries(run)), proj[0][:, run], ADD)
            nc.vector.tensor_tensor(early[:, 1, run], acc[1][:, run], picked_pe[:, run], ADD)
        for c in (1, 2, 3, 0, 4):
            if c == WOVEN:
                nc.scalar.activation(pairs[:, 0], early[:, :, chunks[c]].rearrange("p t n -> p n t"), GELU)
            else:
                gelu_pair(c, 0, early)

        late = tile("late", [P, 2, S], F32)
        nc.vector.tensor_tensor(late[:, 0, :], pe_table[2][:].indirect(offsets[:]), proj[2][:], ADD)
        picked_late = tile("picked_late", [P, SCALAR_RUN.stop - SCALAR_RUN.start], F32)
        nc.scalar.activation(picked_late[:], pe_table[3][:].indirect(entries(SCALAR_RUN)), COPY)
        for run in LATE_RUNS:
            nc.vector.tensor_tensor(late[:, 1, run], pe_table[3][:].indirect(entries(run)), proj[3][:, run], ADD)
        nc.vector.tensor_tensor(late[:, 1, SCALAR_RUN], acc[3][:, SCALAR_RUN], picked_late[:], ADD)
        for c in range(len(CHUNKS)):
            if c == WOVEN:
                nc.scalar.activation(pairs[:, 1], late[:, :, chunks[c]].rearrange("p t n -> p n t"), GELU)
            else:
                gelu_pair(c, 2, late)

        w2_grouped = tile("w2_grouped", [P, N, PACK], BF16)
        nc.vector.tensor_copy(
            w2_grouped[:].rearrange("p (c i) j -> p c j i", i=PACK),
            w2_raw[:].rearrange("p j (c i) -> p c j i", i=PACK),
        )
        nc.vector.tensor_copy(
            hidden[WOVEN][:].rearrange("p n t -> p (n t)").bitcast(F32).rearrange("p (n u) -> p n u", u=2),
            pairs[:].rearrange("p u n t -> p (u n t)").bitcast(F32).rearrange("p (u n) -> p n u", u=2),
        )
        w2_codes = tile("w2_codes", [P, N], U32)
        w2_scales = tile("w2_scales", [P, N], U8)
        h_codes = [tile(f"h_codes{c}", [P, w], U32) for c, w in enumerate(CHUNKS)]
        h_scales = [tile(f"h_scales{c}", [P, w], U8) for c, w in enumerate(CHUNKS)]

        def quantise_h(c):
            nc.vector.quantize_mx(h_codes[c][:].bitcast(FP8X4), h_scales[c][:], hidden[c][:].rearrange("p n t -> p (n t)"))

        quantise_h(0)
        nc.vector.quantize_mx(w2_codes[:].bitcast(FP8X4), w2_scales[:], w2_grouped[:].rearrange("p c j -> p (c j)"))
        quantise_h(1)
        for c in range(2, len(CHUNKS)):
            quantise_h(c)

        result = {}
        for c in (1, 2, 0, 3, 4):
            w = CHUNKS[c]
            res = ps.tile([P, w], F32, name=f"res{c}", tag=f"bank{(PACK + c) % 8}")
            nc.tensor.matmul_mx(
                res[:],
                lhsT=w2_codes[:].bitcast(FP8X4),
                lhsT_scale=w2_scales[:],
                rhs=h_codes[c][:].bitcast(FP8X4),
                rhs_scale=h_scales[c][:],
                start=True,
                stop=True,
            )
            result[c] = res
        ends = tile("staged_ends", [P, 2, CHUNKS[0]], F32)
        staged = {c: tile(f"staged{c}", [P, CHUNKS[c]], F32) for c in (1, 2, 3)}
        nc.scalar.copy(staged[1][:], result[1][:])
        nc.scalar.dma_start(out[:, chunks[1]], staged[1][:])
        nc.vector.tensor_copy(staged[2][:], result[2][:])
        nc.sync.dma_start(out[:, chunks[2]], staged[2][:])
        nc.scalar.copy(ends[:, 1, :], result[0][:])
        nc.scalar.copy(staged[3][:], result[3][:])
        nc.scalar.dma_start(out[:, chunks[3]], staged[3][:])
        nc.vector.tensor_copy(ends[:, 0, :], result[4][:])
        nc.sync.dma_start(out[:, STARTS[4] : S], ends[:].rearrange("p c n -> p (c n)"))
